import numpy as np
import ml_dtypes


def mxq(x, axis, fmt="e4m3"):
    dtype, down = {"e4m3": (ml_dtypes.float8_e4m3fn, 7), "e5m2": (ml_dtypes.float8_e5m2, 14)}[fmt]
    v = np.moveaxis(np.asarray(x, np.float32).astype(ml_dtypes.bfloat16).astype(np.float64), axis, -1)
    blocks = v.reshape(v.shape[:-1] + (-1, 32))
    amax = np.abs(blocks).max(-1, keepdims=True)
    byte = np.maximum(np.where(amax > 0, np.frexp(amax)[1] - 1 + 127, 0) - down, 1)
    scale = np.exp2(byte - 127.0)
    codes = (blocks / scale).astype(np.float32).astype(dtype).astype(np.float64)
    return np.moveaxis((codes * scale).reshape(v.shape), -1, axis)


WIDE = False


def mx_kscale(k):
    if not WIDE:
        return np.ones(k)
    levels = np.array([10, -10, 5, -5, 0])
    if k % 512:
        return np.exp2(np.random.permutation(np.resize(levels, k // 32))).repeat(32)
    a = np.empty((k // 512, 16))
    for p in range(k // 512):
        a[p, :8] = np.random.permutation(np.resize(levels, 8))
        for g in range(8):
            far = levels[np.abs(levels - a[p, g]) >= 10]
            a[p, g + 8] = far[np.random.randint(len(far))]
    return np.exp2(a.ravel()).repeat(32)


BF16 = ml_dtypes.bfloat16


def bf(x):
    return np.asarray(x, np.float32).astype(BF16)


def f64(x):
    return np.asarray(x).astype(np.float64)


T, D, K = 1024, 512, 1024


def neural_features(x, wq, bias):
    return np.tanh((mxq(x, 1, "e4m3") @ wq) + bias[None, :])


def draw0():
    s, t = mx_kscale(D), mx_kscale(T)
    return {
        "x0": bf(np.random.standard_normal((T, D)) * s),
        "x1": bf(np.random.standard_normal((T, D)) * s),
        "w": bf(np.random.standard_normal((D, K)) / np.sqrt(D) / s[:, None]),
        "bias": bf(0.2 * np.random.standard_normal(K)),
        "a": bf(np.exp(0.3 * np.random.standard_normal(T)) * t),
        "b": bf(np.exp(0.3 * np.random.standard_normal(T)) / t),
    }


def core(x0, x1, w, bias, a, b):
    x0, x1, bias, a, b = f64(x0), f64(x1), f64(bias), f64(a), f64(b)
    wq = mxq(f64(w), 0, "e4m3")
    c0 = neural_features(x0, wq, bias)
    c1 = neural_features(x1, wq, bias)
    p = a * b
    z = np.sum(p)
    m0 = np.sum(p[:, None] * c0, axis=0)
    m1 = np.sum(p[:, None] * c1, axis=0)
    left = a[:, None] * c0
    right = b[:, None] * c1
    s = mxq(left, 0, "e4m3").T @ mxq(right, 0, "e4m3")
    return (s - m0[:, None] * m1[None, :] / z) / np.sqrt(z)


def e4m3fn_bytes(y):
    return np.clip(np.asarray(y, np.float64), -448.0, 448.0).astype(np.float32).astype(ml_dtypes.float8_e4m3fn).view(np.uint8)


def e4m3fn_values(b):
    return np.asarray(b, np.uint8).view(ml_dtypes.float8_e4m3fn).astype(np.float64)


def setup_inputs():
    d = draw0()
    x0 = np.asarray(d['x1']).astype(np.float64)
    s = (np.max(np.abs(x0), axis=(0,), keepdims=True) / 448.0).astype(np.float32)
    out = {}
    for k, v in d.items():
        if k == 'x1':
            out['x1_bytes'] = e4m3fn_bytes(x0 / s.astype(np.float64))
            out['x1_scale'] = s
        else:
            out[k] = v
    return out


def reference(x0, x1_bytes, x1_scale, w, bias, a, b):
    return core(x0, e4m3fn_values(x1_bytes) * x1_scale.astype(np.float64), w, bias, a, b)

@@ -1,0 +1,407 @@
+from contextlib import ExitStack
+
+import concourse.mybir as mybir
+from concourse.masks import make_identity
+
+T, D, K = 1024, 512, 1024
+P = 128
+PACK = 4
+GROUP = P * PACK
+NB = K // P
+QW = 256
+
+F32 = mybir.dt.float32
+BF16 = mybir.dt.bfloat16
+U32 = mybir.dt.uint32
+U8 = mybir.dt.uint8
+FP8 = mybir.dt.float8_e4m3fn
+FP8X4 = mybir.dt.float8_e4m3fn_x4
+ALU = mybir.AluOpType
+ACT = mybir.ActivationFunctionType
+
+FLOPS = 2 * 2 * T * D * K + 2 * T * K * K + 2 * 2 * T * K
+
+PATHS = "GGGVGGVGVGVGGGGG"
+RANK_ONE = "GGSGSSGS"
+W_COPY = "VSVV"
+X_COPY = "SSSVSSVS"
+
+
+def operand(s):
+    return 1 - s // NB
+
+
+def tile_girsanovreweightedneurallagcovariance_kernel(
+    tc, x0, x1_bytes, x1_scale, w, bias, a, b, out
+):
+    nc = tc.nc
+    with ExitStack() as ctx:
+        keep = ctx.enter_context(tc.tile_pool(name="keep", bufs=1))
+        work = ctx.enter_context(tc.tile_pool(name="work", bufs=3))
+        tpool = ctx.enter_context(tc.tile_pool(name="tpool", bufs=8))
+        psum = ctx.enter_context(tc.psum_pool(name="psum", bufs=3))
+        psum2 = ctx.enter_context(tc.psum_pool(name="psum2", bufs=2))
+        ctx.enter_context(tc.manual_schedule())
+
+        x0_sb = [keep.tile([P, PACK, D], BF16, name="x0_sb%d" % g, align_bytes=64) for g in range(2)]
+        w_sb = [keep.tile([P, PACK, QW], BF16, name="w_sb%d" % q, align_bytes=64) for q in range(4)]
+        x1_raw = [keep.tile([P, PACK * D], U8, name="x1_raw%d" % g, align_bytes=64) for g in range(2)]
+        sc_bc = keep.tile([P, D], F32, align_bytes=64)
+        ab16 = [keep.tile([P, 2, PACK], BF16, name="ab16_%d" % i) for i in range(2)]
+        bias_rows = keep.tile([P, P], BF16)
+
+        nc.gpsimd.memset(bias_rows[:], 0.0)
+        ident = keep.tile([P, P], F32)
+        make_identity(nc, ident[:])
+        ident16 = keep.tile([P, P], BF16)
+        make_identity(nc, ident16[:])
+        half = keep.tile([P, 1], F32)
+        nc.gpsimd.memset(half[:], -0.5)
+
+        x0_v = x0.rearrange("(g m j) k -> g m j k", g=2, j=PACK)
+        w_v = w.rearrange("(p t) n -> p t n", t=PACK)
+        x1_v = x1_bytes.rearrange("(g m j) k -> g m (j k)", g=2, j=PACK)
+        def load_w(q):
+            nc.sync.dma_start(out=w_sb[q][:], in_=w_v[:, :, q * QW : (q + 1) * QW])
+
+        nc.scalar.dma_start(out=ab16[0][:], in_=a.rearrange("(g m j) -> m g j", g=2, j=PACK))
+        nc.scalar.dma_start(out=ab16[1][:], in_=b.rearrange("(g m j) -> m g j", g=2, j=PACK))
+        nc.scalar.dma_start(out=bias_rows[0:NB, :], in_=bias.rearrange("(b p) -> b p", p=P))
+        load_w(0)
+        nc.sync.dma_start(out=sc_bc[:], in_=x1_scale.rearrange("o k -> (o k)").partition_broadcast(P))
+        nc.sync.dma_start(out=x1_raw[0][:], in_=x1_v[0])
+        nc.sync.dma_start(out=x1_raw[1][:], in_=x1_v[1])
+        load_w(1)
+        load_w(2)
+        load_w(3)
+        nc.sync.dma_start(out=x0_sb[0][:], in_=x0_v[0])
+        nc.sync.dma_start(out=x0_sb[1][:], in_=x0_v[1])
+
+        warm = keep.tile([P, 1], F32)
+        nc.vector.memset(warm[:], 0.0)
+        nc.scalar.activation(out=warm[:], in_=warm[:], func=ACT.Tanh)
+
+        wq = [keep.tile([P, QW], U32, name="wq%d" % q, align_bytes=64) for q in range(4)]
+        ws = [keep.tile([P, QW], U8, name="ws%d" % q, align_bytes=64) for q in range(4)]
+        xq, xs, lq, ls = {}, {}, {}, {}
+        for o in range(2):
+            for g in range(2):
+                xq[o, g] = keep.tile([P, GROUP], U32, name="xq%d%d" % (o, g), align_bytes=64)
+                xs[o, g] = keep.tile([P, GROUP], U8, name="xs%d%d" % (o, g), align_bytes=64)
+                lq[o, g] = keep.tile([P, K], U32, name="lq%d%d" % (o, g), align_bytes=64)
+                ls[o, g] = keep.tile([P, K], U8, name="ls%d%d" % (o, g), align_bytes=64)
+        ab = keep.tile([P, 2, 2, PACK], F32)
+        p4 = keep.tile([P, 2 * PACK], F32)
+        p_bc = keep.tile([P, 2, GROUP], F32)
+        zacc = keep.tile([P, 2], F32)
+        z_sb = keep.tile([P, 1], F32)
+        r_sb = keep.tile([P, 1], F32)
+        zinv = keep.tile([P, 1], F32)
+        nrz = keep.tile([P, 1], F32)
+        bias_col = keep.tile([P, NB], F32)
+        m_col = [keep.tile([P, NB], F32, name="m_col%d" % o) for o in range(2)]
+        m1_bc = keep.tile([P, K], F32)
+
+        def bias_transpose():
+            bank = psum.tile([P, P], BF16, name="tr")
+            nc.tensor.transpose(bank[:], bias_rows[:], ident16[:])
+            nc.scalar.copy(out=bias_col[:], in_=bank[:, 0:NB])
+
+        def weights_a():
+            nc.vector.tensor_copy(out=ab[:, 0], in_=ab16[0][:])
+            nc.vector.tensor_copy(out=ab[:, 1], in_=ab16[1][:])
+            nc.vector.tensor_tensor(
+                out=p4[:],
+                in0=ab[:, 0].rearrange("p g j -> p (g j)"),
+                in1=ab[:, 1].rearrange("p g j -> p (g j)"),
+                op=ALU.mult,
+            )
+
+        def weights_b(g):
+            bank = psum.tile([P, PACK, P], F32, name="tr")
+            for j in range(PACK):
+                col = g * PACK + j
+                nc.tensor.transpose(bank[:, j, :], p4[:, col : col + 1].to_broadcast([P, P]), ident[:])
+            nc.scalar.activation(
+                out=p_bc[:, g, :],
+                in_=bank[:].rearrange("p j m -> p (j m)"),
+                func=ACT.Copy,
+                accum_out=zacc[:, g : g + 1],
+            )
+
+        def normaliser_a():
+            nc.vector.tensor_tensor(out=z_sb[:], in0=zacc[:, 0:1], in1=zacc[:, 1:2], op=ALU.add)
+            nc.gpsimd.tensor_tensor(out=r_sb[:], in0=z_sb[:], in1=half[:], op=ALU.pow)
+
+        def normaliser_b():
+            nc.vector.reciprocal(out=zinv[:], in_=z_sb[:])
+            nc.vector.tensor_scalar(
+                out=nrz[:], in0=zinv[:], scalar1=r_sb[:, 0:1], scalar2=-1.0, op0=ALU.mult, op1=ALU.mult
+            )
+
+        w_grp, x_grp, x_bank, x_wide = {}, {}, {}, {}
+
+        copy = {"V": nc.vector.tensor_copy, "S": nc.scalar.copy}
+
+        def w_interleave(q):
+            engine = copy[W_COPY[q]]
+            w_grp[q] = work.tile([P, QW * PACK], BF16, name="w_grp", align_bytes=64)
+            engine(
+                out=w_grp[q][:].rearrange("p (n t) -> p n t", t=PACK),
+                in_=w_sb[q][:].rearrange("p t n -> p n t"),
+            )
+
+        def w_quantize(q):
+            nc.vector.quantize_mx(out=wq[q][:].bitcast(FP8X4), scales=ws[q][:], in_=w_grp[q][:])
+
+        def x_transpose(o, g, h):
+            rows = x0_sb[g][:].rearrange("p j k -> p (j k)") if o == 0 else x_wide[g][:]
+            words = rows.bitcast(F32)
+            bank = psum.tile([P, 2, 2, P], F32, name="tr")
+            x_bank[o, g, h] = bank
+            for jj in range(2):
+                for u in range(2):
+                    base = (2 * h + jj) * (D // 2)
+                    nc.tensor.transpose(
+                        bank[:, jj, u, :], words[:, base + u : base + D // 2 : 2], ident[:]
+                    )
+
+        def x_copy(o, g, h):
+            engine = copy[X_COPY[4 * (1 - o) + 2 * g + h]]
+            grp = work.tile([P, 2 * P * PACK], BF16, name="x_grp", align_bytes=64)
+            x_grp[o, g, h] = grp
+            engine(
+                out=grp[:].bitcast(F32).rearrange("p (j m u) -> p j m u", j=2, u=2),
+                in_=x_bank[o, g, h][:].rearrange("p j u m -> p j m u"),
+            )
+
+        def x_quantize(o, g, h):
+            cols = slice(2 * h * P, 2 * (h + 1) * P)
+            nc.vector.quantize_mx(
+                out=xq[o, g][:, cols].bitcast(FP8X4), scales=xs[o, g][:, cols], in_=x_grp[o, g, h][:]
+            )
+
+        def x_widen(g, j):
+            if j == 0:
+                x_wide[g] = work.tile([P, PACK * D], BF16, name="x_wide", align_bytes=64)
+            cols = slice(j * D, (j + 1) * D)
+            nc.vector.tensor_tensor(
+                out=x_wide[g][:, cols], in0=x1_raw[g][:, cols].bitcast(FP8), in1=sc_bc[:], op=ALU.mult
+            )
+
+        mm, tr, c_t, pc_t, grp_t = {}, {}, {}, {}, {}
+
+        def features_matmul(s, g):
+            o, fb = operand(s), s % NB
+            f_cols = slice((fb % 2) * P, (fb % 2 + 1) * P)
+            mm[s, g] = psum.tile([P, GROUP], F32, name="mm")
+            nc.tensor.matmul_mx(
+                out=mm[s, g][:],
+                lhsT=wq[fb // 2][:, f_cols].bitcast(FP8X4),
+                lhsT_scale=ws[fb // 2][:, f_cols],
+                rhs=xq[o, g][:].bitcast(FP8X4),
+                rhs_scale=xs[o, g][:],
+                start=True,
+                stop=True,
+            )
+
+        def tanh(s, g):
+            if g == 0:
+                c_t[s] = tpool.tile([P, 2, GROUP], F32, name="c")
+            nc.scalar.activation(
+                out=c_t[s][:, g, :], in_=mm[s, g][:], func=ACT.Tanh, bias=bias_col[:, s % NB : s % NB + 1]
+            )
+
+        def moment_vector(s):
+            o, fb = operand(s), s % NB
+            junk = work.tile([P, 2 * GROUP], F32, name="junk")
+            nc.vector.scalar_tensor_tensor(
+                out=junk[:],
+                in0=c_t[s][:].rearrange("p g t -> p (g t)"),
+                scalar=1.0,
+                in1=p_bc[:].rearrange("p g t -> p (g t)"),
+                op0=ALU.mult,
+                op1=ALU.mult,
+                accum_out=m_col[o][:, fb : fb + 1],
+            )
+
+        def moment_product(s):
+            pc_t[s] = work.tile([P, 2, GROUP], F32, name="pc")
+            for g in range(2):
+                nc.gpsimd.tensor_tensor(
+                    out=pc_t[s][:, g, :], in0=c_t[s][:, g, :], in1=p_bc[:, g, :], op=ALU.mult
+                )
+
+        def moment_sum(s):
+            o, fb = operand(s), s % NB
+            junk = work.tile([P, 2, GROUP], BF16, name="junk_s")
+            nc.scalar.activation(
+                out=junk[:], in_=pc_t[s][:], func=ACT.Copy, accum_out=m_col[o][:, fb : fb + 1]
+            )
+
+        def features_transpose(s, g):
+            tr[s, g] = psum.tile([P, PACK, P], F32, name="tr")
+            for j in range(PACK):
+                nc.tensor.transpose(tr[s, g][:, j, :], c_t[s][:, g, j * P : (j + 1) * P], ident[:])
+
+        def scale(s, g):
+            o = operand(s)
+            grp_t[s, g] = tpool.tile([P, GROUP], BF16, name="grp", align_bytes=64)
+            nc.vector.tensor_tensor(
+                out=grp_t[s, g][:].rearrange("p (f j) -> p f j", j=PACK),
+                in0=tr[s, g][:].rearrange("p j f -> p f j"),
+                in1=ab[:, o, g, :].unsqueeze(1).to_broadcast([P, P, PACK]),
+                op=ALU.mult,
+            )
+
+        def quantize(s, g):
+            o, fb = operand(s), s % NB
+            cols = slice(fb * P, (fb + 1) * P)
+            nc.vector.quantize_mx(
+                out=lq[o, g][:, cols].bitcast(FP8X4), scales=ls[o, g][:, cols], in_=grp_t[s, g][:]
+            )
+
+        tmp_t, acc_t = {}, {}
+
+        def spread_m1(half_k):
+            bank = psum.tile([P, 4, P], F32, name="tr")
+            for n in range(4):
+                fb = 4 * half_k + n
+                nc.tensor.transpose(bank[:, n, :], m_col[1][:, fb : fb + 1].to_broadcast([P, P]), ident[:])
+            nc.scalar.activation(
+                out=m1_bc[:, half_k * GROUP : (half_k + 1) * GROUP],
+                in_=bank[:].rearrange("p n f -> p (n f)"),
+                func=ACT.Copy,
+                scale=nrz[:, 0:1],
+            )
+
+        def rank_one(i, v):
+            if v == 0:
+                tmp_t[i] = work.tile([P, 2, GROUP], F32, name="tmp")
+            src = m1_bc[:, v * GROUP : (v + 1) * GROUP]
+            if RANK_ONE[i] == "G":
+                nc.gpsimd.tensor_scalar(
+                    out=tmp_t[i][:, v, :], in0=src, scalar1=m_col[0][:, i : i + 1], scalar2=0.0,
+                    op0=ALU.mult, op1=ALU.add,
+                )
+            else:
+                nc.scalar.activation(out=tmp_t[i][:, v, :], in_=src, func=ACT.Copy, scale=m_col[0][:, i : i + 1])
+
+        def lag_matmul(i, v):
+            acc_t[i, v] = psum2.tile([P, GROUP], F32, name="acc")
+            rows = slice(i * P, (i + 1) * P)
+            cols = slice(v * GROUP, (v + 1) * GROUP)
+            for g in range(2):
+                nc.tensor.matmul_mx(
+                    out=acc_t[i, v][:],
+                    lhsT=lq[0, g][:, rows].bitcast(FP8X4),
+                    lhsT_scale=ls[0, g][:, rows],
+                    rhs=lq[1, g][:, cols].bitcast(FP8X4),
+                    rhs_scale=ls[1, g][:, cols],
+                    start=(g == 0),
+                    stop=(g == 1),
+                )
+
+        def finish(i, v):
+            res = tpool.tile([P, GROUP], F32, name="res")
+            nc.vector.scalar_tensor_tensor(
+                out=res[:], in0=acc_t[i, v][:], scalar=r_sb[:, 0:1], in1=tmp_t[i][:, v, :],
+                op0=ALU.mult, op1=ALU.add,
+            )
+            nc.sync.dma_start(out=out[i * P : (i + 1) * P, v * GROUP : (v + 1) * GROUP], in_=res[:])
+
+        weights_a()
+        w_interleave(0)
+        bias_transpose()
+        weights_b(0)
+        weights_b(1)
+        x_widen(0, 0)
+        x_widen(0, 1)
+        x_transpose(1, 0, 0)
+        x_copy(1, 0, 0)
+        x_widen(0, 2)
+        w_quantize(0)
+        x_widen(0, 3)
+        x_transpose(1, 0, 1)
+        x_copy(1, 0, 1)
+        x_quantize(1, 0, 0)
+        x_widen(1, 0)
+        x_widen(1, 1)
+        x_transpose(1, 1, 0)
+        x_quantize(1, 0, 1)
+        features_matmul(0, 0)
+        features_matmul(1, 0)
+        tanh(0, 0)
+        x_copy(1, 1, 0)
+        x_widen(1, 2)
+        x_widen(1, 3)
+        x_transpose(1, 1, 1)
+        tanh(1, 0)
+        x_copy(1, 1, 1)
+        x_quantize(1, 1, 0)
+        features_transpose(0, 0)
+        features_transpose(1, 0)
+        normaliser_a()
+        w_interleave(1)
+        x_quantize(1, 1, 1)
+        scale(0, 0)
+        features_matmul(0, 1)
+        features_matmul(1, 1)
+        tanh(0, 1)
+        tanh(1, 1)
+        w_quantize(1)
+        scale(1, 0)
+        features_transpose(0, 1)
+        normaliser_b()
+
+        def extra(s):
+            if s in (2, 4):
+                w_interleave(2 + (s - 2) // 2)
+            if s in (3, 5):
+                w_quantize(2 + (s - 2) // 2)
+            if s in (3, 4, 5, 6):
+                g, h = (s - 3) // 2, (s - 3) % 2
+                x_transpose(0, g, h)
+                x_copy(0, g, h)
+            if s in (4, 5, 6, 7):
+                x_quantize(0, (s - 4) // 2, (s - 4) % 2)
+
+        n_units = 2 * NB
+        for s in range(1, n_units + 6):
+            extra(s)
+            if s + 1 < n_units:
+                features_matmul(s + 1, 0)
+                features_matmul(s + 1, 1)
+            if 1 < s < n_units:
+                tanh(s, 0)
+                tanh(s, 1)
+            if 1 < s - 2 < n_units:
+                scale(s - 2, 0)
+            if 0 <= s - 1 < n_units:
+                if PATHS[s - 1] == "V":
+                    moment_vector(s - 1)
+                else:
+                    moment_product(s - 1)
+                if s - 1 > 1:
+                    features_transpose(s - 1, 0)
+            if 0 <= s - 2 < n_units:
+                scale(s - 2, 1)
+            if 1 <= s - 1 < n_units:
+                features_transpose(s - 1, 1)
+            if 0 <= s - 3 < n_units:
+                if PATHS[s - 3] == "G":
+                    moment_sum(s - 3)
+                quantize(s - 3, 0)
+                quantize(s - 3, 1)
+            if s == NB + 2:
+                spread_m1(0)
+                spread_m1(1)
+            i = s - 3 - NB
+            if 0 <= i < NB:
+                rank_one(i, 0)
+                rank_one(i, 1)
+                lag_matmul(i, 0)
+                lag_matmul(i, 1)
+            if 0 <= i - 1 < NB:
+                finish(i - 1, 0)
+                finish(i - 1, 1)

@@ -21,10 +21,13 @@ ACT = mybir.ActivationFunctionType
 
 FLOPS = 2 * 2 * T * D * K + 2 * T * K * K + 2 * 2 * T * K
 
-PATHS = "GGGVGGVGVGVGGGGG"
-RANK_ONE = "GGSGSSGS"
-W_COPY = "VSVV"
-X_COPY = "SSSVSSVS"
+PATHS = "VVVVGVVVVVVVVGVV"
+RANK_ONE = "SSSSSSSG"
+EVAC = "VVSVVVSVSSVVSVSS"
+GP_COLS = 256
+JOINED = [[(0, 1), (2, 3), (4, 5), (6, 7)], [(0, 1), (2, 3), (4, 5), (6,), (7,)]]
+W_COPY = "VSSS"
+X_COPY = "SSSVSSSS"
 
 
 def operand(s):
@@ -38,6 +41,7 @@ def tile_girsanovreweightedneurallagcovariance_kernel(
     with ExitStack() as ctx:
         keep = ctx.enter_context(tc.tile_pool(name="keep", bufs=1))
         work = ctx.enter_context(tc.tile_pool(name="work", bufs=3))
+        grp_pool = ctx.enter_context(tc.tile_pool(name="grp_pool", bufs=4))
         tpool = ctx.enter_context(tc.tile_pool(name="tpool", bufs=8))
         psum = ctx.enter_context(tc.psum_pool(name="psum", bufs=3))
         psum2 = ctx.enter_context(tc.psum_pool(name="psum2", bufs=2))
@@ -88,8 +92,14 @@ def tile_girsanovreweightedneurallagcovariance_kernel(
             for g in range(2):
                 xq[o, g] = keep.tile([P, GROUP], U32, name="xq%d%d" % (o, g), align_bytes=64)
                 xs[o, g] = keep.tile([P, GROUP], U8, name="xs%d%d" % (o, g), align_bytes=64)
-                lq[o, g] = keep.tile([P, K], U32, name="lq%d%d" % (o, g), align_bytes=64)
-                ls[o, g] = keep.tile([P, K], U8, name="ls%d%d" % (o, g), align_bytes=64)
+        home = {}
+        for o in range(2):
+            for blocks in JOINED[1 - o]:
+                width = len(blocks) * P
+                lq[o, blocks] = keep.tile([P, 2, width], U32, name="lq%d%d" % (o, blocks[0]), align_bytes=64)
+                ls[o, blocks] = keep.tile([P, 2, width], U8, name="ls%d%d" % (o, blocks[0]), align_bytes=64)
+                for n, fb in enumerate(blocks):
+                    home[o, fb] = (blocks, n)
         ab = keep.tile([P, 2, 2, PACK], F32)
         p4 = keep.tile([P, 2 * PACK], F32)
         p_bc = keep.tile([P, 2, GROUP], F32)
@@ -189,7 +199,7 @@ def tile_girsanovreweightedneurallagcovariance_kernel(
                 out=x_wide[g][:, cols], in0=x1_raw[g][:, cols].bitcast(FP8), in1=sc_bc[:], op=ALU.mult
             )
 
-        mm, tr, c_t, pc_t, grp_t = {}, {}, {}, {}, {}
+        mm, tr, c_t, pc_t, grp_t, planar_t = {}, {}, {}, {}, {}, {}
 
         def features_matmul(s, g):
             o, fb = operand(s), s % NB
@@ -228,9 +238,11 @@ def tile_girsanovreweightedneurallagcovariance_kernel(
         def moment_product(s):
             pc_t[s] = work.tile([P, 2, GROUP], F32, name="pc")
             for g in range(2):
-                nc.gpsimd.tensor_tensor(
-                    out=pc_t[s][:, g, :], in0=c_t[s][:, g, :], in1=p_bc[:, g, :], op=ALU.mult
-                )
+                for v in range(0, GROUP, GP_COLS):
+                    cols = slice(v, v + GP_COLS)
+                    nc.gpsimd.tensor_tensor(
+                        out=pc_t[s][:, g, cols], in0=c_t[s][:, g, cols], in1=p_bc[:, g, cols], op=ALU.mult
+                    )
 
         def moment_sum(s):
             o, fb = operand(s), s % NB
@@ -246,20 +258,46 @@ def tile_girsanovreweightedneurallagcovariance_kernel(
 
         def scale(s, g):
             o = operand(s)
-            grp_t[s, g] = tpool.tile([P, GROUP], BF16, name="grp", align_bytes=64)
+            if EVAC[s] == "S":
+                if g == 0:
+                    planar_t[s] = work.tile([P, 2, PACK, P], BF16, name="planar")
+                for j in range(PACK):
+                    nc.scalar.activation(
+                        out=planar_t[s][:, g, j, :], in_=tr[s, g][:, j, :], func=ACT.Copy,
+                        scale=ab[:, o, g, j : j + 1],
+                    )
+                return
             nc.vector.tensor_tensor(
-                out=grp_t[s, g][:].rearrange("p (f j) -> p f j", j=PACK),
+                out=grouped(s, g).rearrange("p (f j) -> p f j", j=PACK),
                 in0=tr[s, g][:].rearrange("p j f -> p f j"),
                 in1=ab[:, o, g, :].unsqueeze(1).to_broadcast([P, P, PACK]),
                 op=ALU.mult,
             )
 
-        def quantize(s, g):
+        def grouped(s, g):
             o, fb = operand(s), s % NB
-            cols = slice(fb * P, (fb + 1) * P)
-            nc.vector.quantize_mx(
-                out=lq[o, g][:, cols].bitcast(FP8X4), scales=ls[o, g][:, cols], in_=grp_t[s, g][:]
-            )
+            blocks, n = home[o, fb]
+            if (o, blocks) not in grp_t:
+                grp_t[o, blocks] = grp_pool.tile([P, 2, len(blocks) * GROUP], BF16, name="grp", align_bytes=64)
+            return grp_t[o, blocks][:, g, n * GROUP : (n + 1) * GROUP]
+
+        def interleave(s):
+            if EVAC[s] == "S":
+                for g in range(2):
+                    nc.vector.tensor_copy(
+                        out=grouped(s, g).rearrange("p (f j) -> p f j", j=PACK),
+                        in_=planar_t[s][:, g].rearrange("p j f -> p f j"),
+                    )
+
+        def quantize(s):
+            o, fb = operand(s), s % NB
+            blocks, n = home[o, fb]
+            if n == len(blocks) - 1:
+                nc.vector.quantize_mx(
+                    out=lq[o, blocks][:].rearrange("p g f -> p (g f)").bitcast(FP8X4),
+                    scales=ls[o, blocks][:].rearrange("p g f -> p (g f)"),
+                    in_=grp_t[o, blocks][:].rearrange("p g f -> p (g f)"),
+                )
 
         tmp_t, acc_t = {}, {}
 
@@ -289,18 +327,19 @@ def tile_girsanovreweightedneurallagcovariance_kernel(
 
         def lag_matmul(i, v):
             acc_t[i, v] = psum2.tile([P, GROUP], F32, name="acc")
-            rows = slice(i * P, (i + 1) * P)
-            cols = slice(v * GROUP, (v + 1) * GROUP)
-            for g in range(2):
-                nc.tensor.matmul_mx(
-                    out=acc_t[i, v][:],
-                    lhsT=lq[0, g][:, rows].bitcast(FP8X4),
-                    lhsT_scale=ls[0, g][:, rows],
-                    rhs=lq[1, g][:, cols].bitcast(FP8X4),
-                    rhs_scale=ls[1, g][:, cols],
-                    start=(g == 0),
-                    stop=(g == 1),
-                )
+            rows, n = home[0, i]
+            for blocks in JOINED[0][2 * v : 2 * v + 2]:
+                first = blocks[0] * P - v * GROUP
+                for g in range(2):
+                    nc.tensor.matmul_mx(
+                        out=acc_t[i, v][:, first : first + 2 * P],
+                        lhsT=lq[0, rows][:, g, n * P : (n + 1) * P].bitcast(FP8X4),
+                        lhsT_scale=ls[0, rows][:, g, n * P : (n + 1) * P],
+                        rhs=lq[1, blocks][:, g, :].bitcast(FP8X4),
+                        rhs_scale=ls[1, blocks][:, g, :],
+                        start=(g == 0),
+                        stop=(g == 1),
+                    )
 
         def finish(i, v):
             res = tpool.tile([P, GROUP], F32, name="res")
@@ -367,7 +406,7 @@ def tile_girsanovreweightedneurallagcovariance_kernel(
                 x_quantize(0, (s - 4) // 2, (s - 4) % 2)
 
         n_units = 2 * NB
-        for s in range(1, n_units + 6):
+        for s in range(1, n_units + 5):
             extra(s)
             if s + 1 < n_units:
                 features_matmul(s + 1, 0)
@@ -391,17 +430,19 @@ def tile_girsanovreweightedneurallagcovariance_kernel(
             if 0 <= s - 3 < n_units:
                 if PATHS[s - 3] == "G":
                     moment_sum(s - 3)
-                quantize(s - 3, 0)
-                quantize(s - 3, 1)
+                interleave(s - 3)
+                quantize(s - 3)
             if s == NB + 2:
                 spread_m1(0)
                 spread_m1(1)
-            i = s - 3 - NB
-            if 0 <= i < NB:
-                rank_one(i, 0)
-                rank_one(i, 1)
-                lag_matmul(i, 0)
-                lag_matmul(i, 1)
-            if 0 <= i - 1 < NB:
-                finish(i - 1, 0)
-                finish(i - 1, 1)
+            if NB <= s - 3 < n_units:
+                rank_one(s - 3 - NB, 0)
+                rank_one(s - 3 - NB, 1)
+            if NB <= s - 4 < n_units:
+                blocks, n = home[0, s - 4 - NB]
+                if n == len(blocks) - 1:
+                    for i in blocks:
+                        lag_matmul(i, 0)
+                        lag_matmul(i, 1)
+                        finish(i, 0)
+                        finish(i, 1)

@@ -17,17 +17,32 @@ U8 = mybir.dt.uint8
 FP8 = mybir.dt.float8_e4m3fn
 FP8X4 = mybir.dt.float8_e4m3fn_x4
 ALU = mybir.AluOpType
+AX = mybir.AxisListType
 ACT = mybir.ActivationFunctionType
 
 FLOPS = 2 * 2 * T * D * K + 2 * T * K * K + 2 * 2 * T * K
 
-PATHS = "VVVVGVVVVVVVVGVV"
-RANK_ONE = "SSSSSSSG"
-EVAC = "VVSVVVSVSSVVSVSS"
-GP_COLS = 256
-JOINED = [[(0, 1), (2, 3), (4, 5), (6, 7)], [(0, 1), (2, 3), (4, 5), (6,), (7,)]]
-W_COPY = "VSSS"
-X_COPY = "SSSVSSSS"
+PRODUCT = "GGGGGVGGVGGVGGGG"
+EVAC = "SSSSSSSSSSSSSSSS"
+RANK_ONE = "GSSSGSGS"
+GP_HALVES = 1
+LAG = 4
+FREE_ACC = 8
+REPEAT = "1111111111111111"
+STEP = "afxrmlt1qpbg"
+JOIN1 = "44"
+JOIN0 = "11111111"
+W_COPY = "VSVS"
+X_CAST = "VVVSSSSS"
+X_COPY = "SSSS"
+
+
+def joined(o):
+    groups, first = [], 0
+    for width in JOIN1 if o == 1 else JOIN0:
+        groups.append(tuple(range(first, first + int(width))))
+        first += int(width)
+    return groups
 
 
 def operand(s):
@@ -43,17 +58,19 @@ def tile_girsanovreweightedneurallagcovariance_kernel(
         work = ctx.enter_context(tc.tile_pool(name="work", bufs=3))
         grp_pool = ctx.enter_context(tc.tile_pool(name="grp_pool", bufs=4))
         tpool = ctx.enter_context(tc.tile_pool(name="tpool", bufs=8))
-        psum = ctx.enter_context(tc.psum_pool(name="psum", bufs=3))
+        psum = ctx.enter_context(tc.psum_pool(name="psum", bufs=2))
+        psum1 = ctx.enter_context(tc.psum_pool(name="psum1", bufs=1))
         psum2 = ctx.enter_context(tc.psum_pool(name="psum2", bufs=2))
         ctx.enter_context(tc.manual_schedule())
 
         x0_sb = [keep.tile([P, PACK, D], BF16, name="x0_sb%d" % g, align_bytes=64) for g in range(2)]
         w_sb = [keep.tile([P, PACK, QW], BF16, name="w_sb%d" % q, align_bytes=64) for q in range(4)]
         x1_raw = [keep.tile([P, PACK * D], U8, name="x1_raw%d" % g, align_bytes=64) for g in range(2)]
-        sc_bc = keep.tile([P, D], F32, align_bytes=64)
+        sc4 = keep.tile([P, PACK], F32)
         ab16 = [keep.tile([P, 2, PACK], BF16, name="ab16_%d" % i) for i in range(2)]
         bias_rows = keep.tile([P, P], BF16)
 
+        a_bc = keep.tile([P, T], BF16)
         nc.gpsimd.memset(bias_rows[:], 0.0)
         ident = keep.tile([P, P], F32)
         make_identity(nc, ident[:])
@@ -70,16 +87,17 @@ def tile_girsanovreweightedneurallagcovariance_kernel(
 
         nc.scalar.dma_start(out=ab16[0][:], in_=a.rearrange("(g m j) -> m g j", g=2, j=PACK))
         nc.scalar.dma_start(out=ab16[1][:], in_=b.rearrange("(g m j) -> m g j", g=2, j=PACK))
+        nc.scalar.dma_start(out=sc4[:], in_=x1_scale.rearrange("o (p t) -> p (o t)", t=PACK))
         nc.scalar.dma_start(out=bias_rows[0:NB, :], in_=bias.rearrange("(b p) -> b p", p=P))
-        load_w(0)
-        nc.sync.dma_start(out=sc_bc[:], in_=x1_scale.rearrange("o k -> (o k)").partition_broadcast(P))
         nc.sync.dma_start(out=x1_raw[0][:], in_=x1_v[0])
+        load_w(0)
         nc.sync.dma_start(out=x1_raw[1][:], in_=x1_v[1])
         load_w(1)
         load_w(2)
         load_w(3)
         nc.sync.dma_start(out=x0_sb[0][:], in_=x0_v[0])
         nc.sync.dma_start(out=x0_sb[1][:], in_=x0_v[1])
+        nc.sync.dma_start(out=a_bc[:], in_=a.partition_broadcast(P))
 
         warm = keep.tile([P, 1], F32)
         nc.vector.memset(warm[:], 0.0)
@@ -94,7 +112,7 @@ def tile_girsanovreweightedneurallagcovariance_kernel(
                 xs[o, g] = keep.tile([P, GROUP], U8, name="xs%d%d" % (o, g), align_bytes=64)
         home = {}
         for o in range(2):
-            for blocks in JOINED[1 - o]:
+            for blocks in joined(o):
                 width = len(blocks) * P
                 lq[o, blocks] = keep.tile([P, 2, width], U32, name="lq%d%d" % (o, blocks[0]), align_bytes=64)
                 ls[o, blocks] = keep.tile([P, 2, width], U8, name="ls%d%d" % (o, blocks[0]), align_bytes=64)
@@ -102,13 +120,15 @@ def tile_girsanovreweightedneurallagcovariance_kernel(
                     home[o, fb] = (blocks, n)
         ab = keep.tile([P, 2, 2, PACK], F32)
         p4 = keep.tile([P, 2 * PACK], F32)
-        p_bc = keep.tile([P, 2, GROUP], F32)
-        zacc = keep.tile([P, 2], F32)
+        b_bc = keep.tile([P, 2, GROUP], F32)
+        p_ps = [psum1.tile([P, 2, P, 2], F32, name="p_ps%d" % g) for g in range(2)]
+        zcol = keep.tile([P, 1], F32)
         z_sb = keep.tile([P, 1], F32)
         r_sb = keep.tile([P, 1], F32)
         zinv = keep.tile([P, 1], F32)
         nrz = keep.tile([P, 1], F32)
         bias_col = keep.tile([P, NB], F32)
+        m_part = [keep.tile([P, NB, 2], F32, name="m_part%d" % o) for o in range(2)]
         m_col = [keep.tile([P, NB], F32, name="m_col%d" % o) for o in range(2)]
         m1_bc = keep.tile([P, K], F32)
 
@@ -127,20 +147,25 @@ def tile_girsanovreweightedneurallagcovariance_kernel(
                 op=ALU.mult,
             )
 
-        def weights_b(g):
-            bank = psum.tile([P, PACK, P], F32, name="tr")
+        def weights_p(g):
             for j in range(PACK):
                 col = g * PACK + j
-                nc.tensor.transpose(bank[:, j, :], p4[:, col : col + 1].to_broadcast([P, P]), ident[:])
-            nc.scalar.activation(
-                out=p_bc[:, g, :],
-                in_=bank[:].rearrange("p j m -> p (j m)"),
-                func=ACT.Copy,
-                accum_out=zacc[:, g : g + 1],
+                nc.tensor.transpose(p_ps[g][:, j // 2, :, j % 2], p4[:, col : col + 1].to_broadcast([P, P]), ident[:])
+
+        def weights_spread(g):
+            bank = psum2.tile([P, PACK, P], F32, name="acc")
+            for j in range(PACK):
+                nc.tensor.transpose(bank[:, j, :], ab[:, 1, g, j : j + 1].to_broadcast([P, P]), ident[:])
+            nc.scalar.copy(
+                out=b_bc[:, g, :].rearrange("p (u m e) -> p u m e", u=2, e=2),
+                in_=bank[:].rearrange("p (u e) m -> p u m e", u=2),
             )
 
         def normaliser_a():
-            nc.vector.tensor_tensor(out=z_sb[:], in0=zacc[:, 0:1], in1=zacc[:, 1:2], op=ALU.add)
+            nc.vector.reduce_sum(out=zcol[:], in_=p4[:], axis=AX.X)
+            bank = psum2.tile([P, P], F32, name="acc")
+            nc.tensor.transpose(bank[:], zcol[:].to_broadcast([P, P]), ident[:])
+            nc.vector.reduce_sum(out=z_sb[:], in_=bank[:], axis=AX.X)
             nc.gpsimd.tensor_tensor(out=r_sb[:], in0=z_sb[:], in1=half[:], op=ALU.pow)
 
         def normaliser_b():
@@ -167,7 +192,8 @@ def tile_girsanovreweightedneurallagcovariance_kernel(
         def x_transpose(o, g, h):
             rows = x0_sb[g][:].rearrange("p j k -> p (j k)") if o == 0 else x_wide[g][:]
             words = rows.bitcast(F32)
-            bank = psum.tile([P, 2, 2, P], F32, name="tr")
+            pool, tag = ((psum, "tr"), (psum2, "acc"))[h]
+            bank = pool.tile([P, 2, 2, P], F32, name=tag)
             x_bank[o, g, h] = bank
             for jj in range(2):
                 for u in range(2):
@@ -177,7 +203,7 @@ def tile_girsanovreweightedneurallagcovariance_kernel(
                     )
 
         def x_copy(o, g, h):
-            engine = copy[X_COPY[4 * (1 - o) + 2 * g + h]]
+            engine = copy[X_COPY[2 * g + h]]
             grp = work.tile([P, 2 * P * PACK], BF16, name="x_grp", align_bytes=64)
             x_grp[o, g, h] = grp
             engine(
@@ -191,103 +217,133 @@ def tile_girsanovreweightedneurallagcovariance_kernel(
                 out=xq[o, g][:, cols].bitcast(FP8X4), scales=xs[o, g][:, cols], in_=x_grp[o, g, h][:]
             )
 
-        def x_widen(g, j):
+        def x_cast(g, j):
             if j == 0:
                 x_wide[g] = work.tile([P, PACK * D], BF16, name="x_wide", align_bytes=64)
             cols = slice(j * D, (j + 1) * D)
-            nc.vector.tensor_tensor(
-                out=x_wide[g][:, cols], in0=x1_raw[g][:, cols].bitcast(FP8), in1=sc_bc[:], op=ALU.mult
-            )
+            copy[X_CAST[PACK * g + j]](out=x_wide[g][:, cols], in_=x1_raw[g][:, cols].bitcast(FP8))
 
-        mm, tr, c_t, pc_t, grp_t, planar_t = {}, {}, {}, {}, {}, {}
+        def x_scale(g, h):
+            grp = work.tile([P, 2 * P * PACK], BF16, name="x_grp", align_bytes=64)
+            x_grp[1, g, h] = grp
+            for jj in range(2):
+                pairs = x_bank[1, g, h][:, jj].rearrange("p u m -> p (u m)").bitcast(BF16)
+                nc.vector.tensor_tensor(
+                    out=grp[:, jj * GROUP : (jj + 1) * GROUP].rearrange("p (m u z) -> p m u z", u=2, z=2),
+                    in0=pairs.rearrange("p (u m z) -> p m u z", u=2, z=2),
+                    in1=sc4[:].rearrange("p (u z) -> p u z", z=2).unsqueeze(1).to_broadcast([P, P, 2, 2]),
+                    op=ALU.mult,
+                )
+
+        mm, tr, c_t, prod_t, grp_t = {}, {}, {}, {}, {}
 
         def features_matmul(s, g):
             o, fb = operand(s), s % NB
             f_cols = slice((fb % 2) * P, (fb % 2 + 1) * P)
-            mm[s, g] = psum.tile([P, GROUP], F32, name="mm")
-            nc.tensor.matmul_mx(
-                out=mm[s, g][:],
-                lhsT=wq[fb // 2][:, f_cols].bitcast(FP8X4),
-                lhsT_scale=ws[fb // 2][:, f_cols],
-                rhs=xq[o, g][:].bitcast(FP8X4),
-                rhs_scale=xs[o, g][:],
-                start=True,
-                stop=True,
-            )
+            if 1 < s < FREE_ACC and s % 2:
+                mm[s, g] = psum2.tile([P, GROUP], F32, name="acc")
+            else:
+                mm[s, g] = psum.tile([P, GROUP], F32, name="mm")
+            for n in range(int(REPEAT[s])):
+                nc.tensor.matmul_mx(
+                    out=mm[s, g][:],
+                    lhsT=wq[fb // 2][:, f_cols].bitcast(FP8X4),
+                    lhsT_scale=ws[fb // 2][:, f_cols],
+                    rhs=xq[o, g][:].bitcast(FP8X4),
+                    rhs_scale=xs[o, g][:],
+                    start=True,
+                    stop=True,
+                )
 
         def tanh(s, g):
             if g == 0:
                 c_t[s] = tpool.tile([P, 2, GROUP], F32, name="c")
             nc.scalar.activation(
-                out=c_t[s][:, g, :], in_=mm[s, g][:], func=ACT.Tanh, bias=bias_col[:, s % NB : s % NB + 1]
+                out=c_t[s][:, g, :].rearrange("p (u m e) -> p u m e", u=2, e=2),
+                in_=mm[s, g][:].rearrange("p (u e m) -> p u m e", u=2, e=2),
+                func=ACT.Tanh,
+                bias=bias_col[:, s % NB : s % NB + 1],
             )
 
-        def moment_vector(s):
+        def moment(s, g):
             o, fb = operand(s), s % NB
-            junk = work.tile([P, 2 * GROUP], F32, name="junk")
+            junk = work.tile([P, GROUP], F32, name="junk")
             nc.vector.scalar_tensor_tensor(
                 out=junk[:],
-                in0=c_t[s][:].rearrange("p g t -> p (g t)"),
+                in0=c_t[s][:, g, :],
                 scalar=1.0,
-                in1=p_bc[:].rearrange("p g t -> p (g t)"),
+                in1=p_ps[g][:].rearrange("p u m e -> p (u m e)"),
                 op0=ALU.mult,
                 op1=ALU.mult,
-                accum_out=m_col[o][:, fb : fb + 1],
+                accum_out=m_part[o][:, fb, g : g + 1],
             )
 
-        def moment_product(s):
-            pc_t[s] = work.tile([P, 2, GROUP], F32, name="pc")
-            for g in range(2):
-                for v in range(0, GROUP, GP_COLS):
-                    cols = slice(v, v + GP_COLS)
-                    nc.gpsimd.tensor_tensor(
-                        out=pc_t[s][:, g, cols], in0=c_t[s][:, g, cols], in1=p_bc[:, g, cols], op=ALU.mult
-                    )
-
-        def moment_sum(s):
-            o, fb = operand(s), s % NB
-            junk = work.tile([P, 2, GROUP], BF16, name="junk_s")
-            nc.scalar.activation(
-                out=junk[:], in_=pc_t[s][:], func=ACT.Copy, accum_out=m_col[o][:, fb : fb + 1]
-            )
-
-        def features_transpose(s, g):
-            tr[s, g] = psum.tile([P, PACK, P], F32, name="tr")
-            for j in range(PACK):
-                nc.tensor.transpose(tr[s, g][:, j, :], c_t[s][:, g, j * P : (j + 1) * P], ident[:])
-
-        def scale(s, g):
-            o = operand(s)
-            if EVAC[s] == "S":
-                if g == 0:
-                    planar_t[s] = work.tile([P, 2, PACK, P], BF16, name="planar")
-                for j in range(PACK):
-                    nc.scalar.activation(
-                        out=planar_t[s][:, g, j, :], in_=tr[s, g][:, j, :], func=ACT.Copy,
-                        scale=ab[:, o, g, j : j + 1],
-                    )
-                return
+        def moment_total(o, first, last):
             nc.vector.tensor_tensor(
-                out=grouped(s, g).rearrange("p (f j) -> p f j", j=PACK),
-                in0=tr[s, g][:].rearrange("p j f -> p f j"),
-                in1=ab[:, o, g, :].unsqueeze(1).to_broadcast([P, P, PACK]),
-                op=ALU.mult,
+                out=m_col[o][:, first:last],
+                in0=m_part[o][:, first:last, 0],
+                in1=m_part[o][:, first:last, 1],
+                op=ALU.add,
             )
 
-        def grouped(s, g):
+        def product(s, g):
+            o = operand(s)
+            if PRODUCT[s] == "V":
+                return
+            if g == 0:
+                prod_t[s] = tpool.tile([P, 2, GROUP], BF16, name="prod")
+            for u in range(0, 2, GP_HALVES):
+                cols = slice(u * GROUP // 2, (u + GP_HALVES) * GROUP // 2)
+                if o == 1:
+                    weights = b_bc[:, g, cols]
+                else:
+                    weights = a_bc[:, g * GROUP : (g + 1) * GROUP].rearrange("p (m u e) -> p u m e", u=2, e=2)
+                    weights = weights[:, u : u + GP_HALVES]
+                nc.gpsimd.tensor_tensor(
+                    out=shaped(prod_t[s][:, g, cols], o),
+                    in0=shaped(c_t[s][:, g, cols], o),
+                    in1=weights,
+                    op=ALU.mult,
+                )
+
+        def shaped(row, o):
+            return row if o == 1 else row.rearrange("p (u m e) -> p u m e", u=GP_HALVES, e=2)
+
+        def product_transpose(s):
+            if PRODUCT[s] == "V":
+                for g in range(2):
+                    tr[s, g] = psum.tile([P, PACK, P], F32, name="tr")
+                    for j in range(PACK):
+                        first = j // 2 * 2 * P + j % 2
+                        nc.tensor.transpose(tr[s, g][:, j, :], c_t[s][:, g, first : first + 2 * P - 1 : 2], ident[:])
+                return
+            tr[s] = psum.tile([P, 2, 2, P], F32, name="tr")
+            words = prod_t[s][:].rearrange("p g t -> p (g t)").bitcast(F32)
+            for g in range(2):
+                for u in range(2):
+                    first = (2 * g + u) * P
+                    nc.tensor.transpose(tr[s][:, g, u, :], words[:, first : first + P], ident[:])
+
+        def grouping(s):
             o, fb = operand(s), s % NB
             blocks, n = home[o, fb]
-            if (o, blocks) not in grp_t:
+            if n == 0:
                 grp_t[o, blocks] = grp_pool.tile([P, 2, len(blocks) * GROUP], BF16, name="grp", align_bytes=64)
-            return grp_t[o, blocks][:, g, n * GROUP : (n + 1) * GROUP]
-
-        def interleave(s):
-            if EVAC[s] == "S":
+            if PRODUCT[s] == "V":
                 for g in range(2):
-                    nc.vector.tensor_copy(
-                        out=grouped(s, g).rearrange("p (f j) -> p f j", j=PACK),
-                        in_=planar_t[s][:, g].rearrange("p j f -> p f j"),
+                    nc.vector.tensor_tensor(
+                        out=grp_t[o, blocks][:, g, n * GROUP : (n + 1) * GROUP].rearrange("p (f j) -> p f j", j=PACK),
+                        in0=tr[s, g][:].rearrange("p j f -> p f j"),
+                        in1=ab[:, o, g, :].unsqueeze(1).to_broadcast([P, P, PACK]),
+                        op=ALU.mult,
                     )
+                return
+            words = grp_t[o, blocks][:].bitcast(F32)
+            half_w = GROUP // 2
+            copy[EVAC[s]](
+                out=words[:, :, n * half_w : (n + 1) * half_w].rearrange("p g (f u) -> p g f u", u=2),
+                in_=tr[s][:].rearrange("p g u f -> p g f u"),
+            )
 
         def quantize(s):
             o, fb = operand(s), s % NB
@@ -302,7 +358,7 @@ def tile_girsanovreweightedneurallagcovariance_kernel(
         tmp_t, acc_t = {}, {}
 
         def spread_m1(half_k):
-            bank = psum.tile([P, 4, P], F32, name="tr")
+            bank = psum2.tile([P, 4, P], F32, name="acc")
             for n in range(4):
                 fb = 4 * half_k + n
                 nc.tensor.transpose(bank[:, n, :], m_col[1][:, fb : fb + 1].to_broadcast([P, P]), ident[:])
@@ -315,7 +371,7 @@ def tile_girsanovreweightedneurallagcovariance_kernel(
 
         def rank_one(i, v):
             if v == 0:
-                tmp_t[i] = work.tile([P, 2, GROUP], F32, name="tmp")
+                tmp_t[i] = tpool.tile([P, 2, GROUP], F32, name="tmp")
             src = m1_bc[:, v * GROUP : (v + 1) * GROUP]
             if RANK_ONE[i] == "G":
                 nc.gpsimd.tensor_scalar(
@@ -328,11 +384,13 @@ def tile_girsanovreweightedneurallagcovariance_kernel(
         def lag_matmul(i, v):
             acc_t[i, v] = psum2.tile([P, GROUP], F32, name="acc")
             rows, n = home[0, i]
-            for blocks in JOINED[0][2 * v : 2 * v + 2]:
+            for blocks in joined(1):
+                if blocks[0] // 4 != v:
+                    continue
                 first = blocks[0] * P - v * GROUP
                 for g in range(2):
                     nc.tensor.matmul_mx(
-                        out=acc_t[i, v][:, first : first + 2 * P],
+                        out=acc_t[i, v][:, first : first + len(blocks) * P],
                         lhsT=lq[0, rows][:, g, n * P : (n + 1) * P].bitcast(FP8X4),
                         lhsT_scale=ls[0, rows][:, g, n * P : (n + 1) * P],
                         rhs=lq[1, blocks][:, g, :].bitcast(FP8X4),
@@ -349,100 +407,107 @@ def tile_girsanovreweightedneurallagcovariance_kernel(
             )
             nc.sync.dma_start(out=out[i * P : (i + 1) * P, v * GROUP : (v + 1) * GROUP], in_=res[:])
 
+        for j in range(PACK):
+            x_cast(0, j)
         weights_a()
         w_interleave(0)
-        bias_transpose()
-        weights_b(0)
-        weights_b(1)
-        x_widen(0, 0)
-        x_widen(0, 1)
         x_transpose(1, 0, 0)
-        x_copy(1, 0, 0)
-        x_widen(0, 2)
-        w_quantize(0)
-        x_widen(0, 3)
+        x_scale(0, 0)
+        bias_transpose()
         x_transpose(1, 0, 1)
-        x_copy(1, 0, 1)
+        w_quantize(0)
+        x_scale(0, 1)
         x_quantize(1, 0, 0)
-        x_widen(1, 0)
-        x_widen(1, 1)
+        for j in range(PACK):
+            x_cast(1, j)
+        weights_spread(0)
         x_transpose(1, 1, 0)
         x_quantize(1, 0, 1)
         features_matmul(0, 0)
         features_matmul(1, 0)
         tanh(0, 0)
-        x_copy(1, 1, 0)
-        x_widen(1, 2)
-        x_widen(1, 3)
+        x_scale(1, 0)
         x_transpose(1, 1, 1)
+        weights_spread(1)
+        product(0, 0)
         tanh(1, 0)
-        x_copy(1, 1, 1)
-        x_quantize(1, 1, 0)
-        features_transpose(0, 0)
-        features_transpose(1, 0)
-        normaliser_a()
+        x_scale(1, 1)
         w_interleave(1)
+        x_quantize(1, 1, 0)
         x_quantize(1, 1, 1)
-        scale(0, 0)
+        product(1, 0)
+        weights_p(0)
+        weights_p(1)
         features_matmul(0, 1)
         features_matmul(1, 1)
         tanh(0, 1)
         tanh(1, 1)
+        product(0, 1)
+        moment(0, 0)
         w_quantize(1)
-        scale(1, 0)
-        features_transpose(0, 1)
-        normaliser_b()
+        product(1, 1)
 
         def extra(s):
-            if s in (2, 4):
-                w_interleave(2 + (s - 2) // 2)
-            if s in (3, 5):
-                w_quantize(2 + (s - 2) // 2)
+            if s in (1, 2):
+                w_interleave(1 + s)
+            if s in (2, 3):
+                w_quantize(s)
             if s in (3, 4, 5, 6):
                 g, h = (s - 3) // 2, (s - 3) % 2
                 x_transpose(0, g, h)
                 x_copy(0, g, h)
             if s in (4, 5, 6, 7):
                 x_quantize(0, (s - 4) // 2, (s - 4) % 2)
+            if s == 4:
+                normaliser_a()
+            if s == 6:
+                normaliser_b()
 
         n_units = 2 * NB
-        for s in range(1, n_units + 5):
-            extra(s)
-            if s + 1 < n_units:
+
+        def part(what, s):
+            if what == "x":
+                extra(s)
+            if what == "m" and s + 1 < n_units:
                 features_matmul(s + 1, 0)
                 features_matmul(s + 1, 1)
-            if 1 < s < n_units:
+            if what == "t" and 1 < s < n_units:
                 tanh(s, 0)
                 tanh(s, 1)
-            if 1 < s - 2 < n_units:
-                scale(s - 2, 0)
-            if 0 <= s - 1 < n_units:
-                if PATHS[s - 1] == "V":
-                    moment_vector(s - 1)
-                else:
-                    moment_product(s - 1)
-                if s - 1 > 1:
-                    features_transpose(s - 1, 0)
-            if 0 <= s - 2 < n_units:
-                scale(s - 2, 1)
-            if 1 <= s - 1 < n_units:
-                features_transpose(s - 1, 1)
-            if 0 <= s - 3 < n_units:
-                if PATHS[s - 3] == "G":
-                    moment_sum(s - 3)
-                interleave(s - 3)
+            if what == "p" and 1 < s < n_units:
+                product(s, 0)
+                product(s, 1)
+            if what in "ab" and 0 <= s - 1 < n_units and s - 1 + "ab".index(what) > 0:
+                moment(s - 1, "ab".index(what))
+                if what == "b" and NB <= s - 1:
+                    moment_total(0, s - 1 - NB, s - NB)
+                if what == "b" and s == NB:
+                    moment_total(1, 0, NB)
+            if what == "r" and 0 <= s - 2 < n_units:
+                product_transpose(s - 2)
+            if what == "g" and 0 <= s - 2 < n_units:
+                grouping(s - 2)
+            if what == "q" and 0 <= s - 3 < n_units:
                 quantize(s - 3)
-            if s == NB + 2:
+            if what == "1" and s == NB + 2:
                 spread_m1(0)
                 spread_m1(1)
-            if NB <= s - 3 < n_units:
-                rank_one(s - 3 - NB, 0)
-                rank_one(s - 3 - NB, 1)
-            if NB <= s - 4 < n_units:
-                blocks, n = home[0, s - 4 - NB]
-                if n == len(blocks) - 1:
-                    for i in blocks:
-                        lag_matmul(i, 0)
-                        lag_matmul(i, 1)
-                        finish(i, 0)
-                        finish(i, 1)
+            if what == "f":
+                while waiting:
+                    finish(*waiting.pop(0))
+            for i in range(NB):
+                lag_step = max(NB + LAG + i, NB + home[0, i][0][-1] + 3)
+                if what == "1" and s == lag_step - 1:
+                    rank_one(i, 0)
+                    rank_one(i, 1)
+                if what == "l" and s == lag_step:
+                    for v in range(2):
+                        if waiting:
+                            finish(*waiting.pop(0))
+                        lag_matmul(i, v)
+                    waiting.extend([(i, 0), (i, 1)])
+
+        waiting = []
+        for s in range(1, n_units + 6):
+            for what in STEP:
+                part(what, s)

@@ -22,19 +22,20 @@ ACT = mybir.ActivationFunctionType
 
 FLOPS = 2 * 2 * T * D * K + 2 * T * K * K + 2 * 2 * T * K
 
-PRODUCT = "GGGGGVGGVGGVGGGG"
-EVAC = "SSSSSSSSSSSSSSSS"
-RANK_ONE = "GSSSGSGS"
-GP_HALVES = 1
+PRODUCT = "GGGVGGVGGGVGGGVG"
+EVAC = "VSSSSVVSSVSSSSSS"
+RANK_ONE = "SSSSSSGS"
+GP_COLS = "4488884844484884"
 LAG = 4
-FREE_ACC = 8
+OFF = "3232333333232333"
+FREE_ACC = 10
 REPEAT = "1111111111111111"
-STEP = "afxrmlt1qpbg"
-JOIN1 = "44"
-JOIN0 = "11111111"
+STEP = "axtq1fbrmgpl"
+JOIN1 = "224"
+JOIN0 = "2111111"
 W_COPY = "VSVS"
-X_CAST = "VVVSSSSS"
-X_COPY = "SSSS"
+X_CAST = "VSVSSSVS"
+X_COPY = "SSVS"
 
 
 def joined(o):
@@ -70,7 +71,6 @@ def tile_girsanovreweightedneurallagcovariance_kernel(
         ab16 = [keep.tile([P, 2, PACK], BF16, name="ab16_%d" % i) for i in range(2)]
         bias_rows = keep.tile([P, P], BF16)
 
-        a_bc = keep.tile([P, T], BF16)
         nc.gpsimd.memset(bias_rows[:], 0.0)
         ident = keep.tile([P, P], F32)
         make_identity(nc, ident[:])
@@ -97,7 +97,6 @@ def tile_girsanovreweightedneurallagcovariance_kernel(
         load_w(3)
         nc.sync.dma_start(out=x0_sb[0][:], in_=x0_v[0])
         nc.sync.dma_start(out=x0_sb[1][:], in_=x0_v[1])
-        nc.sync.dma_start(out=a_bc[:], in_=a.partition_broadcast(P))
 
         warm = keep.tile([P, 1], F32)
         nc.vector.memset(warm[:], 0.0)
@@ -120,7 +119,7 @@ def tile_girsanovreweightedneurallagcovariance_kernel(
                     home[o, fb] = (blocks, n)
         ab = keep.tile([P, 2, 2, PACK], F32)
         p4 = keep.tile([P, 2 * PACK], F32)
-        b_bc = keep.tile([P, 2, GROUP], F32)
+        wt_bc = [keep.tile([P, 2, GROUP], F32, name="wt_bc%d" % o) for o in range(2)]
         p_ps = [psum1.tile([P, 2, P, 2], F32, name="p_ps%d" % g) for g in range(2)]
         zcol = keep.tile([P, 1], F32)
         z_sb = keep.tile([P, 1], F32)
@@ -147,22 +146,24 @@ def tile_girsanovreweightedneurallagcovariance_kernel(
                 op=ALU.mult,
             )
 
+        def weights_sum():
+            nc.vector.reduce_sum(out=zcol[:], in_=p4[:], axis=AX.X)
+
         def weights_p(g):
             for j in range(PACK):
                 col = g * PACK + j
                 nc.tensor.transpose(p_ps[g][:, j // 2, :, j % 2], p4[:, col : col + 1].to_broadcast([P, P]), ident[:])
 
-        def weights_spread(g):
+        def weights_spread(o, g):
             bank = psum2.tile([P, PACK, P], F32, name="acc")
             for j in range(PACK):
-                nc.tensor.transpose(bank[:, j, :], ab[:, 1, g, j : j + 1].to_broadcast([P, P]), ident[:])
+                nc.tensor.transpose(bank[:, j, :], ab[:, o, g, j : j + 1].to_broadcast([P, P]), ident[:])
             nc.scalar.copy(
-                out=b_bc[:, g, :].rearrange("p (u m e) -> p u m e", u=2, e=2),
+                out=wt_bc[o][:, g, :].rearrange("p (u m e) -> p u m e", u=2, e=2),
                 in_=bank[:].rearrange("p (u e) m -> p u m e", u=2),
             )
 
         def normaliser_a():
-            nc.vector.reduce_sum(out=zcol[:], in_=p4[:], axis=AX.X)
             bank = psum2.tile([P, P], F32, name="acc")
             nc.tensor.transpose(bank[:], zcol[:].to_broadcast([P, P]), ident[:])
             nc.vector.reduce_sum(out=z_sb[:], in_=bank[:], axis=AX.X)
@@ -235,7 +236,7 @@ def tile_girsanovreweightedneurallagcovariance_kernel(
                     op=ALU.mult,
                 )
 
-        mm, tr, c_t, prod_t, grp_t = {}, {}, {}, {}, {}
+        mm, tr, c_t, prod_t, grp_t, ready = {}, {}, {}, {}, {}, {}
 
         def features_matmul(s, g):
             o, fb = operand(s), s % NB
@@ -288,29 +289,23 @@ def tile_girsanovreweightedneurallagcovariance_kernel(
 
         def product(s, g):
             o = operand(s)
-            if PRODUCT[s] == "V":
+            if PRODUCT[s] != "G":
                 return
             if g == 0:
-                prod_t[s] = tpool.tile([P, 2, GROUP], BF16, name="prod")
-            for u in range(0, 2, GP_HALVES):
-                cols = slice(u * GROUP // 2, (u + GP_HALVES) * GROUP // 2)
-                if o == 1:
-                    weights = b_bc[:, g, cols]
-                else:
-                    weights = a_bc[:, g * GROUP : (g + 1) * GROUP].rearrange("p (m u e) -> p u m e", u=2, e=2)
-                    weights = weights[:, u : u + GP_HALVES]
-                nc.gpsimd.tensor_tensor(
-                    out=shaped(prod_t[s][:, g, cols], o),
-                    in0=shaped(c_t[s][:, g, cols], o),
-                    in1=weights,
-                    op=ALU.mult,
-                )
-
-        def shaped(row, o):
-            return row if o == 1 else row.rearrange("p (u m e) -> p u m e", u=GP_HALVES, e=2)
+                prod_t[s] = tpool.tile([P, 2 * GROUP], BF16, name="prod")
+            width = int(GP_COLS[s]) * P
+            for first in range(0, 2 * GROUP, width):
+                cols = slice(first, first + width)
+                if (first + width - 1) // GROUP == g:
+                    nc.gpsimd.tensor_tensor(
+                        out=prod_t[s][:, cols],
+                        in0=c_t[s][:].rearrange("p g t -> p (g t)")[:, cols],
+                        in1=wt_bc[o][:].rearrange("p g t -> p (g t)")[:, cols],
+                        op=ALU.mult,
+                    )
 
         def product_transpose(s):
-            if PRODUCT[s] == "V":
+            if PRODUCT[s] != "G":
                 for g in range(2):
                     tr[s, g] = psum.tile([P, PACK, P], F32, name="tr")
                     for j in range(PACK):
@@ -318,7 +313,7 @@ def tile_girsanovreweightedneurallagcovariance_kernel(
                         nc.tensor.transpose(tr[s, g][:, j, :], c_t[s][:, g, first : first + 2 * P - 1 : 2], ident[:])
                 return
             tr[s] = psum.tile([P, 2, 2, P], F32, name="tr")
-            words = prod_t[s][:].rearrange("p g t -> p (g t)").bitcast(F32)
+            words = prod_t[s][:].bitcast(F32)
             for g in range(2):
                 for u in range(2):
                     first = (2 * g + u) * P
@@ -327,9 +322,21 @@ def tile_girsanovreweightedneurallagcovariance_kernel(
         def grouping(s):
             o, fb = operand(s), s % NB
             blocks, n = home[o, fb]
-            if n == 0:
+            if (o, blocks) not in grp_t:
                 grp_t[o, blocks] = grp_pool.tile([P, 2, len(blocks) * GROUP], BF16, name="grp", align_bytes=64)
-            if PRODUCT[s] == "V":
+            if PRODUCT[s] != "G":
+                if PRODUCT[s] == "D":
+                    planar = work.tile([P, 2, PACK, P], BF16, name="planar")
+                    for g in range(2):
+                        for j in range(PACK):
+                            nc.scalar.activation(
+                                out=planar[:, g, j, :], in_=tr[s, g][:, j, :], func=ACT.Copy, scale=ab[:, o, g, j : j + 1]
+                            )
+                    nc.vector.tensor_copy(
+                        out=grp_t[o, blocks][:, :, n * GROUP : (n + 1) * GROUP].rearrange("p g (f j) -> p g f j", j=PACK),
+                        in_=planar[:].rearrange("p g j f -> p g f j"),
+                    )
+                    return
                 for g in range(2):
                     nc.vector.tensor_tensor(
                         out=grp_t[o, blocks][:, g, n * GROUP : (n + 1) * GROUP].rearrange("p (f j) -> p f j", j=PACK),
@@ -348,7 +355,8 @@ def tile_girsanovreweightedneurallagcovariance_kernel(
         def quantize(s):
             o, fb = operand(s), s % NB
             blocks, n = home[o, fb]
-            if n == len(blocks) - 1:
+            ready[o, blocks] = ready.get((o, blocks), 0) + 1
+            if ready[o, blocks] == len(blocks):
                 nc.vector.quantize_mx(
                     out=lq[o, blocks][:].rearrange("p g f -> p (g f)").bitcast(FP8X4),
                     scales=ls[o, blocks][:].rearrange("p g f -> p (g f)"),
@@ -411,6 +419,7 @@ def tile_girsanovreweightedneurallagcovariance_kernel(
             x_cast(0, j)
         weights_a()
         w_interleave(0)
+        weights_sum()
         x_transpose(1, 0, 0)
         x_scale(0, 0)
         bias_transpose()
@@ -420,31 +429,31 @@ def tile_girsanovreweightedneurallagcovariance_kernel(
         x_quantize(1, 0, 0)
         for j in range(PACK):
             x_cast(1, j)
-        weights_spread(0)
+        weights_spread(1, 0)
         x_transpose(1, 1, 0)
+        x_transpose(1, 1, 1)
         x_quantize(1, 0, 1)
+        x_scale(1, 0)
+        w_interleave(1)
         features_matmul(0, 0)
         features_matmul(1, 0)
         tanh(0, 0)
-        x_scale(1, 0)
-        x_transpose(1, 1, 1)
-        weights_spread(1)
-        product(0, 0)
-        tanh(1, 0)
         x_scale(1, 1)
-        w_interleave(1)
+        tanh(1, 0)
+        product(0, 0)
         x_quantize(1, 1, 0)
         x_quantize(1, 1, 1)
+        w_quantize(1)
         product(1, 0)
         weights_p(0)
-        weights_p(1)
         features_matmul(0, 1)
         features_matmul(1, 1)
+        weights_spread(1, 1)
         tanh(0, 1)
+        weights_p(1)
         tanh(1, 1)
-        product(0, 1)
         moment(0, 0)
-        w_quantize(1)
+        product(0, 1)
         product(1, 1)
 
         def extra(s):
@@ -458,6 +467,8 @@ def tile_girsanovreweightedneurallagcovariance_kernel(
                 x_copy(0, g, h)
             if s in (4, 5, 6, 7):
                 x_quantize(0, (s - 4) // 2, (s - 4) % 2)
+            if s in (6, 8):
+                weights_spread(0, (s - 6) // 2)
             if s == 4:
                 normaliser_a()
             if s == 6:
@@ -483,12 +494,15 @@ def tile_girsanovreweightedneurallagcovariance_kernel(
                     moment_total(0, s - 1 - NB, s - NB)
                 if what == "b" and s == NB:
                     moment_total(1, 0, NB)
-            if what == "r" and 0 <= s - 2 < n_units:
-                product_transpose(s - 2)
-            if what == "g" and 0 <= s - 2 < n_units:
-                grouping(s - 2)
-            if what == "q" and 0 <= s - 3 < n_units:
-                quantize(s - 3)
+            for d in (3, 2):
+                if 0 <= s - d < n_units and d == int(OFF[s - d]):
+                    if what == "r":
+                        product_transpose(s - d)
+                    if what == "g":
+                        grouping(s - d)
+            for d in (4, 3):
+                if what == "q" and 0 <= s - d < n_units and d == int(OFF[s - d]) + 1:
+                    quantize(s - d)
             if what == "1" and s == NB + 2:
                 spread_m1(0)
                 spread_m1(1)
@@ -496,7 +510,7 @@ def tile_girsanovreweightedneurallagcovariance_kernel(
                 while waiting:
                     finish(*waiting.pop(0))
             for i in range(NB):
-                lag_step = max(NB + LAG + i, NB + home[0, i][0][-1] + 3)
+                lag_step = max(NB + LAG + i, max(NB + fb + int(OFF[NB + fb]) + 1 for fb in home[0, i][0]))
                 if what == "1" and s == lag_step - 1:
                     rank_one(i, 0)
                     rank_one(i, 1)
@@ -508,6 +522,6 @@ def tile_girsanovreweightedneurallagcovariance_kernel(
                     waiting.extend([(i, 0), (i, 1)])
 
         waiting = []
-        for s in range(1, n_units + 6):
+        for s in range(1, n_units + 7):
             for what in STEP:
                 part(what, s)

@@ -8,7 +8,7 @@ P = 128
 PACK = 4
 GROUP = P * PACK
 NB = K // P
-QW = 256
+W_CUTS = (0, 256, 512, 1024)
 
 F32 = mybir.dt.float32
 BF16 = mybir.dt.bfloat16
@@ -22,20 +22,19 @@ ACT = mybir.ActivationFunctionType
 
 FLOPS = 2 * 2 * T * D * K + 2 * T * K * K + 2 * 2 * T * K
 
-PRODUCT = "GGGVGGVGGGVGGGVG"
-EVAC = "VSSSSVVSSVSSSSSS"
-RANK_ONE = "SSSSSSGS"
-GP_COLS = "4488884844484884"
-LAG = 4
-OFF = "3232333333232333"
+PRODUCT = "GGVGVGGGGVGGGGGG"
+EVAC = "SSSSSSSSSSSSSSSS"
+RANK_ONE = "SSSSSSSS"
+GP_COLS = "4884448884888888"
+LAG = 5
+OFF = "3322222322332322"
 FREE_ACC = 10
-REPEAT = "1111111111111111"
-STEP = "axtq1fbrmgpl"
-JOIN1 = "224"
-JOIN0 = "2111111"
-W_COPY = "VSVS"
-X_CAST = "VSVSSSVS"
-X_COPY = "SSVS"
+STEP = "txp1afqrbglm"
+JOIN1 = "422"
+JOIN0 = "221111"
+W_COPY = "SSV"
+X_CAST = "VVSS"
+X_COPY = "SVSS"
 
 
 def joined(o):
@@ -58,14 +57,15 @@ def tile_girsanovreweightedneurallagcovariance_kernel(
         keep = ctx.enter_context(tc.tile_pool(name="keep", bufs=1))
         work = ctx.enter_context(tc.tile_pool(name="work", bufs=3))
         grp_pool = ctx.enter_context(tc.tile_pool(name="grp_pool", bufs=4))
-        tpool = ctx.enter_context(tc.tile_pool(name="tpool", bufs=8))
+        tpool = ctx.enter_context(tc.tile_pool(name="tpool", bufs=6))
         psum = ctx.enter_context(tc.psum_pool(name="psum", bufs=2))
         psum1 = ctx.enter_context(tc.psum_pool(name="psum1", bufs=1))
         psum2 = ctx.enter_context(tc.psum_pool(name="psum2", bufs=2))
         ctx.enter_context(tc.manual_schedule())
 
         x0_sb = [keep.tile([P, PACK, D], BF16, name="x0_sb%d" % g, align_bytes=64) for g in range(2)]
-        w_sb = [keep.tile([P, PACK, QW], BF16, name="w_sb%d" % q, align_bytes=64) for q in range(4)]
+        w_width = [W_CUTS[q + 1] - W_CUTS[q] for q in range(3)]
+        w_sb = [keep.tile([P, PACK, w_width[q]], BF16, name="w_sb%d" % q, align_bytes=64) for q in range(3)]
         x1_raw = [keep.tile([P, PACK * D], U8, name="x1_raw%d" % g, align_bytes=64) for g in range(2)]
         sc4 = keep.tile([P, PACK], F32)
         ab16 = [keep.tile([P, 2, PACK], BF16, name="ab16_%d" % i) for i in range(2)]
@@ -83,18 +83,17 @@ def tile_girsanovreweightedneurallagcovariance_kernel(
         w_v = w.rearrange("(p t) n -> p t n", t=PACK)
         x1_v = x1_bytes.rearrange("(g m j) k -> g m (j k)", g=2, j=PACK)
         def load_w(q):
-            nc.sync.dma_start(out=w_sb[q][:], in_=w_v[:, :, q * QW : (q + 1) * QW])
+            nc.sync.dma_start(out=w_sb[q][:], in_=w_v[:, :, W_CUTS[q] : W_CUTS[q + 1]])
 
+        nc.scalar.dma_start(out=sc4[:], in_=x1_scale.rearrange("o (p t) -> p (o t)", t=PACK))
         nc.scalar.dma_start(out=ab16[0][:], in_=a.rearrange("(g m j) -> m g j", g=2, j=PACK))
         nc.scalar.dma_start(out=ab16[1][:], in_=b.rearrange("(g m j) -> m g j", g=2, j=PACK))
-        nc.scalar.dma_start(out=sc4[:], in_=x1_scale.rearrange("o (p t) -> p (o t)", t=PACK))
         nc.scalar.dma_start(out=bias_rows[0:NB, :], in_=bias.rearrange("(b p) -> b p", p=P))
         nc.sync.dma_start(out=x1_raw[0][:], in_=x1_v[0])
         load_w(0)
         nc.sync.dma_start(out=x1_raw[1][:], in_=x1_v[1])
         load_w(1)
         load_w(2)
-        load_w(3)
         nc.sync.dma_start(out=x0_sb[0][:], in_=x0_v[0])
         nc.sync.dma_start(out=x0_sb[1][:], in_=x0_v[1])
 
@@ -102,8 +101,8 @@ def tile_girsanovreweightedneurallagcovariance_kernel(
         nc.vector.memset(warm[:], 0.0)
         nc.scalar.activation(out=warm[:], in_=warm[:], func=ACT.Tanh)
 
-        wq = [keep.tile([P, QW], U32, name="wq%d" % q, align_bytes=64) for q in range(4)]
-        ws = [keep.tile([P, QW], U8, name="ws%d" % q, align_bytes=64) for q in range(4)]
+        wq = [keep.tile([P, w_width[q]], U32, name="wq%d" % q, align_bytes=64) for q in range(3)]
+        ws = [keep.tile([P, w_width[q]], U8, name="ws%d" % q, align_bytes=64) for q in range(3)]
         xq, xs, lq, ls = {}, {}, {}, {}
         for o in range(2):
             for g in range(2):
@@ -181,7 +180,7 @@ def tile_girsanovreweightedneurallagcovariance_kernel(
 
         def w_interleave(q):
             engine = copy[W_COPY[q]]
-            w_grp[q] = work.tile([P, QW * PACK], BF16, name="w_grp", align_bytes=64)
+            w_grp[q] = keep.tile([P, w_width[q] * PACK], BF16, name="w_grp%d" % q, align_bytes=64)
             engine(
                 out=w_grp[q][:].rearrange("p (n t) -> p n t", t=PACK),
                 in_=w_sb[q][:].rearrange("p t n -> p n t"),
@@ -205,28 +204,27 @@ def tile_girsanovreweightedneurallagcovariance_kernel(
 
         def x_copy(o, g, h):
             engine = copy[X_COPY[2 * g + h]]
-            grp = work.tile([P, 2 * P * PACK], BF16, name="x_grp", align_bytes=64)
-            x_grp[o, g, h] = grp
+            if h == 0:
+                x_grp[o, g] = work.tile([P, 4 * P * PACK], BF16, name="x_grp", align_bytes=64)
+            grp = x_grp[o, g][:, 2 * h * GROUP : 2 * (h + 1) * GROUP]
             engine(
-                out=grp[:].bitcast(F32).rearrange("p (j m u) -> p j m u", j=2, u=2),
+                out=grp.bitcast(F32).rearrange("p (j m u) -> p j m u", j=2, u=2),
                 in_=x_bank[o, g, h][:].rearrange("p j u m -> p j m u"),
             )
 
-        def x_quantize(o, g, h):
-            cols = slice(2 * h * P, 2 * (h + 1) * P)
-            nc.vector.quantize_mx(
-                out=xq[o, g][:, cols].bitcast(FP8X4), scales=xs[o, g][:, cols], in_=x_grp[o, g, h][:]
-            )
+        def x_quantize(o, g):
+            nc.vector.quantize_mx(out=xq[o, g][:].bitcast(FP8X4), scales=xs[o, g][:], in_=x_grp[o, g][:])
 
-        def x_cast(g, j):
-            if j == 0:
+        def x_cast(g, first, last, engine):
+            if first == 0:
                 x_wide[g] = work.tile([P, PACK * D], BF16, name="x_wide", align_bytes=64)
-            cols = slice(j * D, (j + 1) * D)
-            copy[X_CAST[PACK * g + j]](out=x_wide[g][:, cols], in_=x1_raw[g][:, cols].bitcast(FP8))
+            cols = slice(first * D, last * D)
+            copy[engine](out=x_wide[g][:, cols], in_=x1_raw[g][:, cols].bitcast(FP8))
 
         def x_scale(g, h):
-            grp = work.tile([P, 2 * P * PACK], BF16, name="x_grp", align_bytes=64)
-            x_grp[1, g, h] = grp
+            if h == 0:
+                x_grp[1, g] = work.tile([P, 4 * P * PACK], BF16, name="x_grp", align_bytes=64)
+            grp = x_grp[1, g][:, 2 * h * GROUP : 2 * (h + 1) * GROUP]
             for jj in range(2):
                 pairs = x_bank[1, g, h][:, jj].rearrange("p u m -> p (u m)").bitcast(BF16)
                 nc.vector.tensor_tensor(
@@ -240,21 +238,21 @@ def tile_girsanovreweightedneurallagcovariance_kernel(
 
         def features_matmul(s, g):
             o, fb = operand(s), s % NB
-            f_cols = slice((fb % 2) * P, (fb % 2 + 1) * P)
+            q = min(fb // 2, 2)
+            f_cols = slice(fb * P - W_CUTS[q], (fb + 1) * P - W_CUTS[q])
             if 1 < s < FREE_ACC and s % 2:
                 mm[s, g] = psum2.tile([P, GROUP], F32, name="acc")
             else:
                 mm[s, g] = psum.tile([P, GROUP], F32, name="mm")
-            for n in range(int(REPEAT[s])):
-                nc.tensor.matmul_mx(
-                    out=mm[s, g][:],
-                    lhsT=wq[fb // 2][:, f_cols].bitcast(FP8X4),
-                    lhsT_scale=ws[fb // 2][:, f_cols],
-                    rhs=xq[o, g][:].bitcast(FP8X4),
-                    rhs_scale=xs[o, g][:],
-                    start=True,
-                    stop=True,
-                )
+            nc.tensor.matmul_mx(
+                out=mm[s, g][:],
+                lhsT=wq[q][:, f_cols].bitcast(FP8X4),
+                lhsT_scale=ws[q][:, f_cols],
+                rhs=xq[o, g][:].bitcast(FP8X4),
+                rhs_scale=xs[o, g][:],
+                start=True,
+                stop=True,
+            )
 
         def tanh(s, g):
             if g == 0:
@@ -377,17 +375,15 @@ def tile_girsanovreweightedneurallagcovariance_kernel(
                 scale=nrz[:, 0:1],
             )
 
-        def rank_one(i, v):
-            if v == 0:
-                tmp_t[i] = tpool.tile([P, 2, GROUP], F32, name="tmp")
-            src = m1_bc[:, v * GROUP : (v + 1) * GROUP]
+        def rank_one(i):
+            tmp_t[i] = tpool.tile([P, 2, GROUP], F32, name="tmp")
+            row = tmp_t[i][:].rearrange("p v t -> p (v t)")
             if RANK_ONE[i] == "G":
                 nc.gpsimd.tensor_scalar(
-                    out=tmp_t[i][:, v, :], in0=src, scalar1=m_col[0][:, i : i + 1], scalar2=0.0,
-                    op0=ALU.mult, op1=ALU.add,
+                    out=row, in0=m1_bc[:], scalar1=m_col[0][:, i : i + 1], scalar2=0.0, op0=ALU.mult, op1=ALU.add
                 )
             else:
-                nc.scalar.activation(out=tmp_t[i][:, v, :], in_=src, func=ACT.Copy, scale=m_col[0][:, i : i + 1])
+                nc.scalar.activation(out=row, in_=m1_bc[:], func=ACT.Copy, scale=m_col[0][:, i : i + 1])
 
         def lag_matmul(i, v):
             acc_t[i, v] = psum2.tile([P, GROUP], F32, name="acc")
@@ -416,7 +412,7 @@ def tile_girsanovreweightedneurallagcovariance_kernel(
             nc.sync.dma_start(out=out[i * P : (i + 1) * P, v * GROUP : (v + 1) * GROUP], in_=res[:])
 
         for j in range(PACK):
-            x_cast(0, j)
+            x_cast(0, j, j + 1, X_CAST[j])
         weights_a()
         w_interleave(0)
         weights_sum()
@@ -426,13 +422,12 @@ def tile_girsanovreweightedneurallagcovariance_kernel(
         x_transpose(1, 0, 1)
         w_quantize(0)
         x_scale(0, 1)
-        x_quantize(1, 0, 0)
-        for j in range(PACK):
-            x_cast(1, j)
+        x_cast(1, 0, 2, "S")
+        x_cast(1, 2, 4, "S")
         weights_spread(1, 0)
         x_transpose(1, 1, 0)
+        x_quantize(1, 0)
         x_transpose(1, 1, 1)
-        x_quantize(1, 0, 1)
         x_scale(1, 0)
         w_interleave(1)
         features_matmul(0, 0)
@@ -441,9 +436,8 @@ def tile_girsanovreweightedneurallagcovariance_kernel(
         x_scale(1, 1)
         tanh(1, 0)
         product(0, 0)
-        x_quantize(1, 1, 0)
-        x_quantize(1, 1, 1)
         w_quantize(1)
+        x_quantize(1, 1)
         product(1, 0)
         weights_p(0)
         features_matmul(0, 1)
@@ -457,16 +451,16 @@ def tile_girsanovreweightedneurallagcovariance_kernel(
         product(1, 1)
 
         def extra(s):
-            if s in (1, 2):
-                w_interleave(1 + s)
-            if s in (2, 3):
-                w_quantize(s)
+            if s == 1:
+                w_interleave(2)
+            if s == 2:
+                w_quantize(2)
             if s in (3, 4, 5, 6):
                 g, h = (s - 3) // 2, (s - 3) % 2
                 x_transpose(0, g, h)
                 x_copy(0, g, h)
-            if s in (4, 5, 6, 7):
-                x_quantize(0, (s - 4) // 2, (s - 4) % 2)
+            if s in (5, 7):
+                x_quantize(0, (s - 5) // 2)
             if s in (6, 8):
                 weights_spread(0, (s - 6) // 2)
             if s == 4:
@@ -490,8 +484,8 @@ def tile_girsanovreweightedneurallagcovariance_kernel(
                 product(s, 1)
             if what in "ab" and 0 <= s - 1 < n_units and s - 1 + "ab".index(what) > 0:
                 moment(s - 1, "ab".index(what))
-                if what == "b" and NB <= s - 1:
-                    moment_total(0, s - 1 - NB, s - NB)
+                if what == "b" and NB <= s - 1 and (s % 2 == 0 or s - 1 == n_units - 2):
+                    moment_total(0, s - 2 + s % 2 - NB if s < n_units else s - 1 - NB, s - NB)
                 if what == "b" and s == NB:
                     moment_total(1, 0, NB)
             for d in (3, 2):
@@ -512,8 +506,7 @@ def tile_girsanovreweightedneurallagcovariance_kernel(
             for i in range(NB):
                 lag_step = max(NB + LAG + i, max(NB + fb + int(OFF[NB + fb]) + 1 for fb in home[0, i][0]))
                 if what == "1" and s == lag_step - 1:
-                    rank_one(i, 0)
-                    rank_one(i, 1)
+                    rank_one(i)
                 if what == "l" and s == lag_step:
                     for v in range(2):
                         if waiting:

from contextlib import ExitStack

import concourse.mybir as mybir
from concourse.masks import make_identity

T, D, K = 1024, 512, 1024
P = 128
PACK = 4
GROUP = P * PACK
NB = K // P
W_CUTS = (0, 256, 512, 1024)

F32 = mybir.dt.float32
BF16 = mybir.dt.bfloat16
U32 = mybir.dt.uint32
U8 = mybir.dt.uint8
FP8 = mybir.dt.float8_e4m3fn
FP8X4 = mybir.dt.float8_e4m3fn_x4
ALU = mybir.AluOpType
AX = mybir.AxisListType
ACT = mybir.ActivationFunctionType

FLOPS = 2 * 2 * T * D * K + 2 * T * K * K + 2 * 2 * T * K

PRODUCT = "GGVGVGGGGVGGGGGG"
EVAC = "SSSSSSSSSSSSSSSS"
RANK_ONE = "SSSSSSSS"
GP_COLS = "4884448884888888"
LAG = 5
OFF = "3322222322332322"
FREE_ACC = 10
STEP = "txp1afqrbglm"
JOIN1 = "422"
JOIN0 = "221111"
W_COPY = "SSV"
X_CAST = "VVSS"
X_COPY = "SVSS"


def joined(o):
    groups, first = [], 0
    for width in JOIN1 if o == 1 else JOIN0:
        groups.append(tuple(range(first, first + int(width))))
        first += int(width)
    return groups


def operand(s):
    return 1 - s // NB


def tile_girsanovreweightedneurallagcovariance_kernel(
    tc, x0, x1_bytes, x1_scale, w, bias, a, b, out
):
    nc = tc.nc
    with ExitStack() as ctx:
        keep = ctx.enter_context(tc.tile_pool(name="keep", bufs=1))
        work = ctx.enter_context(tc.tile_pool(name="work", bufs=3))
        grp_pool = ctx.enter_context(tc.tile_pool(name="grp_pool", bufs=4))
        tpool = ctx.enter_context(tc.tile_pool(name="tpool", bufs=6))
        psum = ctx.enter_context(tc.psum_pool(name="psum", bufs=2))
        psum1 = ctx.enter_context(tc.psum_pool(name="psum1", bufs=1))
        psum2 = ctx.enter_context(tc.psum_pool(name="psum2", bufs=2))
        ctx.enter_context(tc.manual_schedule())

        x0_sb = [keep.tile([P, PACK, D], BF16, name="x0_sb%d" % g, align_bytes=64) for g in range(2)]
        w_width = [W_CUTS[q + 1] - W_CUTS[q] for q in range(3)]
        w_sb = [keep.tile([P, PACK, w_width[q]], BF16, name="w_sb%d" % q, align_bytes=64) for q in range(3)]
        x1_raw = [keep.tile([P, PACK * D], U8, name="x1_raw%d" % g, align_bytes=64) for g in range(2)]
        sc4 = keep.tile([P, PACK], F32)
        ab16 = [keep.tile([P, 2, PACK], BF16, name="ab16_%d" % i) for i in range(2)]
        bias_rows = keep.tile([P, P], BF16)

        nc.gpsimd.memset(bias_rows[:], 0.0)
        ident = keep.tile([P, P], F32)
        make_identity(nc, ident[:])
        ident16 = keep.tile([P, P], BF16)
        make_identity(nc, ident16[:])
        half = keep.tile([P, 1], F32)
        nc.gpsimd.memset(half[:], -0.5)

        x0_v = x0.rearrange("(g m j) k -> g m j k", g=2, j=PACK)
        w_v = w.rearrange("(p t) n -> p t n", t=PACK)
        x1_v = x1_bytes.rearrange("(g m j) k -> g m (j k)", g=2, j=PACK)
        def load_w(q):
            nc.sync.dma_start(out=w_sb[q][:], in_=w_v[:, :, W_CUTS[q] : W_CUTS[q + 1]])

        nc.scalar.dma_start(out=sc4[:], in_=x1_scale.rearrange("o (p t) -> p (o t)", t=PACK))
        nc.scalar.dma_start(out=ab16[0][:], in_=a.rearrange("(g m j) -> m g j", g=2, j=PACK))
        nc.scalar.dma_start(out=ab16[1][:], in_=b.rearrange("(g m j) -> m g j", g=2, j=PACK))
        nc.scalar.dma_start(out=bias_rows[0:NB, :], in_=bias.rearrange("(b p) -> b p", p=P))
        nc.sync.dma_start(out=x1_raw[0][:], in_=x1_v[0])
        load_w(0)
        nc.sync.dma_start(out=x1_raw[1][:], in_=x1_v[1])
        load_w(1)
        load_w(2)
        nc.sync.dma_start(out=x0_sb[0][:], in_=x0_v[0])
        nc.sync.dma_start(out=x0_sb[1][:], in_=x0_v[1])

        warm = keep.tile([P, 1], F32)
        nc.vector.memset(warm[:], 0.0)
        nc.scalar.activation(out=warm[:], in_=warm[:], func=ACT.Tanh)

        wq = [keep.tile([P, w_width[q]], U32, name="wq%d" % q, align_bytes=64) for q in range(3)]
        ws = [keep.tile([P, w_width[q]], U8, name="ws%d" % q, align_bytes=64) for q in range(3)]
        xq, xs, lq, ls = {}, {}, {}, {}
        for o in range(2):
            for g in range(2):
                xq[o, g] = keep.tile([P, GROUP], U32, name="xq%d%d" % (o, g), align_bytes=64)
                xs[o, g] = keep.tile([P, GROUP], U8, name="xs%d%d" % (o, g), align_bytes=64)
        home = {}
        for o in range(2):
            for blocks in joined(o):
                width = len(blocks) * P
                lq[o, blocks] = keep.tile([P, 2, width], U32, name="lq%d%d" % (o, blocks[0]), align_bytes=64)
                ls[o, blocks] = keep.tile([P, 2, width], U8, name="ls%d%d" % (o, blocks[0]), align_bytes=64)
                for n, fb in enumerate(blocks):
                    home[o, fb] = (blocks, n)
        ab = keep.tile([P, 2, 2, PACK], F32)
        p4 = keep.tile([P, 2 * PACK], F32)
        wt_bc = [keep.tile([P, 2, GROUP], F32, name="wt_bc%d" % o) for o in range(2)]
        p_ps = [psum1.tile([P, 2, P, 2], F32, name="p_ps%d" % g) for g in range(2)]
        zcol = keep.tile([P, 1], F32)
        z_sb = keep.tile([P, 1], F32)
        r_sb = keep.tile([P, 1], F32)
        zinv = keep.tile([P, 1], F32)
        nrz = keep.tile([P, 1], F32)
        bias_col = keep.tile([P, NB], F32)
        m_part = [keep.tile([P, NB, 2], F32, name="m_part%d" % o) for o in range(2)]
        m_col = [keep.tile([P, NB], F32, name="m_col%d" % o) for o in range(2)]
        m1_bc = keep.tile([P, K], F32)

        def bias_transpose():
            bank = psum.tile([P, P], BF16, name="tr")
            nc.tensor.transpose(bank[:], bias_rows[:], ident16[:])
            nc.scalar.copy(out=bias_col[:], in_=bank[:, 0:NB])

        def weights_a():
            nc.vector.tensor_copy(out=ab[:, 0], in_=ab16[0][:])
            nc.vector.tensor_copy(out=ab[:, 1], in_=ab16[1][:])
            nc.vector.tensor_tensor(
                out=p4[:],
                in0=ab[:, 0].rearrange("p g j -> p (g j)"),
                in1=ab[:, 1].rearrange("p g j -> p (g j)"),
                op=ALU.mult,
            )

        def weights_sum():
            nc.vector.reduce_sum(out=zcol[:], in_=p4[:], axis=AX.X)

        def weights_p(g):
            for j in range(PACK):
                col = g * PACK + j
                nc.tensor.transpose(p_ps[g][:, j // 2, :, j % 2], p4[:, col : col + 1].to_broadcast([P, P]), ident[:])

        def weights_spread(o, g):
            bank = psum2.tile([P, PACK, P], F32, name="acc")
            for j in range(PACK):
                nc.tensor.transpose(bank[:, j, :], ab[:, o, g, j : j + 1].to_broadcast([P, P]), ident[:])
            nc.scalar.copy(
                out=wt_bc[o][:, g, :].rearrange("p (u m e) -> p u m e", u=2, e=2),
                in_=bank[:].rearrange("p (u e) m -> p u m e", u=2),
            )

        def normaliser_a():
            bank = psum2.tile([P, P], F32, name="acc")
            nc.tensor.transpose(bank[:], zcol[:].to_broadcast([P, P]), ident[:])
            nc.vector.reduce_sum(out=z_sb[:], in_=bank[:], axis=AX.X)
            nc.gpsimd.tensor_tensor(out=r_sb[:], in0=z_sb[:], in1=half[:], op=ALU.pow)

        def normaliser_b():
            nc.vector.reciprocal(out=zinv[:], in_=z_sb[:])
            nc.vector.tensor_scalar(
                out=nrz[:], in0=zinv[:], scalar1=r_sb[:, 0:1], scalar2=-1.0, op0=ALU.mult, op1=ALU.mult
            )

        w_grp, x_grp, x_bank, x_wide = {}, {}, {}, {}

        copy = {"V": nc.vector.tensor_copy, "S": nc.scalar.copy}

        def w_interleave(q):
            engine = copy[W_COPY[q]]
            w_grp[q] = keep.tile([P, w_width[q] * PACK], BF16, name="w_grp%d" % q, align_bytes=64)
            engine(
                out=w_grp[q][:].rearrange("p (n t) -> p n t", t=PACK),
                in_=w_sb[q][:].rearrange("p t n -> p n t"),
            )

        def w_quantize(q):
            nc.vector.quantize_mx(out=wq[q][:].bitcast(FP8X4), scales=ws[q][:], in_=w_grp[q][:])

        def x_transpose(o, g, h):
            rows = x0_sb[g][:].rearrange("p j k -> p (j k)") if o == 0 else x_wide[g][:]
            words = rows.bitcast(F32)
            pool, tag = ((psum, "tr"), (psum2, "acc"))[h]
            bank = pool.tile([P, 2, 2, P], F32, name=tag)
            x_bank[o, g, h] = bank
            for jj in range(2):
                for u in range(2):
                    base = (2 * h + jj) * (D // 2)
                    nc.tensor.transpose(
                        bank[:, jj, u, :], words[:, base + u : base + D // 2 : 2], ident[:]
                    )

        def x_copy(o, g, h):
            engine = copy[X_COPY[2 * g + h]]
            if h == 0:
                x_grp[o, g] = work.tile([P, 4 * P * PACK], BF16, name="x_grp", align_bytes=64)
            grp = x_grp[o, g][:, 2 * h * GROUP : 2 * (h + 1) * GROUP]
            engine(
                out=grp.bitcast(F32).rearrange("p (j m u) -> p j m u", j=2, u=2),
                in_=x_bank[o, g, h][:].rearrange("p j u m -> p j m u"),
            )

        def x_quantize(o, g):
            nc.vector.quantize_mx(out=xq[o, g][:].bitcast(FP8X4), scales=xs[o, g][:], in_=x_grp[o, g][:])

        def x_cast(g, first, last, engine):
            if first == 0:
                x_wide[g] = work.tile([P, PACK * D], BF16, name="x_wide", align_bytes=64)
            cols = slice(first * D, last * D)
            copy[engine](out=x_wide[g][:, cols], in_=x1_raw[g][:, cols].bitcast(FP8))

        def x_scale(g, h):
            if h == 0:
                x_grp[1, g] = work.tile([P, 4 * P * PACK], BF16, name="x_grp", align_bytes=64)
            grp = x_grp[1, g][:, 2 * h * GROUP : 2 * (h + 1) * GROUP]
            for jj in range(2):
                pairs = x_bank[1, g, h][:, jj].rearrange("p u m -> p (u m)").bitcast(BF16)
                nc.vector.tensor_tensor(
                    out=grp[:, jj * GROUP : (jj + 1) * GROUP].rearrange("p (m u z) -> p m u z", u=2, z=2),
                    in0=pairs.rearrange("p (u m z) -> p m u z", u=2, z=2),
                    in1=sc4[:].rearrange("p (u z) -> p u z", z=2).unsqueeze(1).to_broadcast([P, P, 2, 2]),
                    op=ALU.mult,
                )

        mm, tr, c_t, prod_t, grp_t, ready = {}, {}, {}, {}, {}, {}

        def features_matmul(s, g):
            o, fb = operand(s), s % NB
            q = min(fb // 2, 2)
            f_cols = slice(fb * P - W_CUTS[q], (fb + 1) * P - W_CUTS[q])
            if 1 < s < FREE_ACC and s % 2:
                mm[s, g] = psum2.tile([P, GROUP], F32, name="acc")
            else:
                mm[s, g] = psum.tile([P, GROUP], F32, name="mm")
            nc.tensor.matmul_mx(
                out=mm[s, g][:],
                lhsT=wq[q][:, f_cols].bitcast(FP8X4),
                lhsT_scale=ws[q][:, f_cols],
                rhs=xq[o, g][:].bitcast(FP8X4),
                rhs_scale=xs[o, g][:],
                start=True,
                stop=True,
            )

        def tanh(s, g):
            if g == 0:
                c_t[s] = tpool.tile([P, 2, GROUP], F32, name="c")
            nc.scalar.activation(
                out=c_t[s][:, g, :].rearrange("p (u m e) -> p u m e", u=2, e=2),
                in_=mm[s, g][:].rearrange("p (u e m) -> p u m e", u=2, e=2),
                func=ACT.Tanh,
                bias=bias_col[:, s % NB : s % NB + 1],
            )

        def moment(s, g):
            o, fb = operand(s), s % NB
            junk = work.tile([P, GROUP], F32, name="junk")
            nc.vector.scalar_tensor_tensor(
                out=junk[:],
                in0=c_t[s][:, g, :],
                scalar=1.0,
                in1=p_ps[g][:].rearrange("p u m e -> p (u m e)"),
                op0=ALU.mult,
                op1=ALU.mult,
                accum_out=m_part[o][:, fb, g : g + 1],
            )

        def moment_total(o, first, last):
            nc.vector.tensor_tensor(
                out=m_col[o][:, first:last],
                in0=m_part[o][:, first:last, 0],
                in1=m_part[o][:, first:last, 1],
                op=ALU.add,
            )

        def product(s, g):
            o = operand(s)
            if PRODUCT[s] != "G":
                return
            if g == 0:
                prod_t[s] = tpool.tile([P, 2 * GROUP], BF16, name="prod")
            width = int(GP_COLS[s]) * P
            for first in range(0, 2 * GROUP, width):
                cols = slice(first, first + width)
                if (first + width - 1) // GROUP == g:
                    nc.gpsimd.tensor_tensor(
                        out=prod_t[s][:, cols],
                        in0=c_t[s][:].rearrange("p g t -> p (g t)")[:, cols],
                        in1=wt_bc[o][:].rearrange("p g t -> p (g t)")[:, cols],
                        op=ALU.mult,
                    )

        def product_transpose(s):
            if PRODUCT[s] != "G":
                for g in range(2):
                    tr[s, g] = psum.tile([P, PACK, P], F32, name="tr")
                    for j in range(PACK):
                        first = j // 2 * 2 * P + j % 2
                        nc.tensor.transpose(tr[s, g][:, j, :], c_t[s][:, g, first : first + 2 * P - 1 : 2], ident[:])
                return
            tr[s] = psum.tile([P, 2, 2, P], F32, name="tr")
            words = prod_t[s][:].bitcast(F32)
            for g in range(2):
                for u in range(2):
                    first = (2 * g + u) * P
                    nc.tensor.transpose(tr[s][:, g, u, :], words[:, first : first + P], ident[:])

        def grouping(s):
            o, fb = operand(s), s % NB
            blocks, n = home[o, fb]
            if (o, blocks) not in grp_t:
                grp_t[o, blocks] = grp_pool.tile([P, 2, len(blocks) * GROUP], BF16, name="grp", align_bytes=64)
            if PRODUCT[s] != "G":
                if PRODUCT[s] == "D":
                    planar = work.tile([P, 2, PACK, P], BF16, name="planar")
                    for g in range(2):
                        for j in range(PACK):
                            nc.scalar.activation(
                                out=planar[:, g, j, :], in_=tr[s, g][:, j, :], func=ACT.Copy, scale=ab[:, o, g, j : j + 1]
                            )
                    nc.vector.tensor_copy(
                        out=grp_t[o, blocks][:, :, n * GROUP : (n + 1) * GROUP].rearrange("p g (f j) -> p g f j", j=PACK),
                        in_=planar[:].rearrange("p g j f -> p g f j"),
                    )
                    return
                for g in range(2):
                    nc.vector.tensor_tensor(
                        out=grp_t[o, blocks][:, g, n * GROUP : (n + 1) * GROUP].rearrange("p (f j) -> p f j", j=PACK),
                        in0=tr[s, g][:].rearrange("p j f -> p f j"),
                        in1=ab[:, o, g, :].unsqueeze(1).to_broadcast([P, P, PACK]),
                        op=ALU.mult,
                    )
                return
            words = grp_t[o, blocks][:].bitcast(F32)
            half_w = GROUP // 2
            copy[EVAC[s]](
                out=words[:, :, n * half_w : (n + 1) * half_w].rearrange("p g (f u) -> p g f u", u=2),
                in_=tr[s][:].rearrange("p g u f -> p g f u"),
            )

        def quantize(s):
            o, fb = operand(s), s % NB
            blocks, n = home[o, fb]
            ready[o, blocks] = ready.get((o, blocks), 0) + 1
            if ready[o, blocks] == len(blocks):
                nc.vector.quantize_mx(
                    out=lq[o, blocks][:].rearrange("p g f -> p (g f)").bitcast(FP8X4),
                    scales=ls[o, blocks][:].rearrange("p g f -> p (g f)"),
                    in_=grp_t[o, blocks][:].rearrange("p g f -> p (g f)"),
                )

        tmp_t, acc_t = {}, {}

        def spread_m1(half_k):
            bank = psum2.tile([P, 4, P], F32, name="acc")
            for n in range(4):
                fb = 4 * half_k + n
                nc.tensor.transpose(bank[:, n, :], m_col[1][:, fb : fb + 1].to_broadcast([P, P]), ident[:])
            nc.scalar.activation(
                out=m1_bc[:, half_k * GROUP : (half_k + 1) * GROUP],
                in_=bank[:].rearrange("p n f -> p (n f)"),
                func=ACT.Copy,
                scale=nrz[:, 0:1],
            )

        def rank_one(i):
            tmp_t[i] = tpool.tile([P, 2, GROUP], F32, name="tmp")
            row = tmp_t[i][:].rearrange("p v t -> p (v t)")
            if RANK_ONE[i] == "G":
                nc.gpsimd.tensor_scalar(
                    out=row, in0=m1_bc[:], scalar1=m_col[0][:, i : i + 1], scalar2=0.0, op0=ALU.mult, op1=ALU.add
                )
            else:
                nc.scalar.activation(out=row, in_=m1_bc[:], func=ACT.Copy, scale=m_col[0][:, i : i + 1])

        def lag_matmul(i, v):
            acc_t[i, v] = psum2.tile([P, GROUP], F32, name="acc")
            rows, n = home[0, i]
            for blocks in joined(1):
                if blocks[0] // 4 != v:
                    continue
                first = blocks[0] * P - v * GROUP
                for g in range(2):
                    nc.tensor.matmul_mx(
                        out=acc_t[i, v][:, first : first + len(blocks) * P],
                        lhsT=lq[0, rows][:, g, n * P : (n + 1) * P].bitcast(FP8X4),
                        lhsT_scale=ls[0, rows][:, g, n * P : (n + 1) * P],
                        rhs=lq[1, blocks][:, g, :].bitcast(FP8X4),
                        rhs_scale=ls[1, blocks][:, g, :],
                        start=(g == 0),
                        stop=(g == 1),
                    )

        def finish(i, v):
            res = tpool.tile([P, GROUP], F32, name="res")
            nc.vector.scalar_tensor_tensor(
                out=res[:], in0=acc_t[i, v][:], scalar=r_sb[:, 0:1], in1=tmp_t[i][:, v, :],
                op0=ALU.mult, op1=ALU.add,
            )
            nc.sync.dma_start(out=out[i * P : (i + 1) * P, v * GROUP : (v + 1) * GROUP], in_=res[:])

        for j in range(PACK):
            x_cast(0, j, j + 1, X_CAST[j])
        weights_a()
        w_interleave(0)
        weights_sum()
        x_transpose(1, 0, 0)
        x_scale(0, 0)
        bias_transpose()
        x_transpose(1, 0, 1)
        w_quantize(0)
        x_scale(0, 1)
        x_cast(1, 0, 2, "S")
        x_cast(1, 2, 4, "S")
        weights_spread(1, 0)
        x_transpose(1, 1, 0)
        x_quantize(1, 0)
        x_transpose(1, 1, 1)
        x_scale(1, 0)
        w_interleave(1)
        features_matmul(0, 0)
        features_matmul(1, 0)
        tanh(0, 0)
        x_scale(1, 1)
        tanh(1, 0)
        product(0, 0)
        w_quantize(1)
        x_quantize(1, 1)
        product(1, 0)
        weights_p(0)
        features_matmul(0, 1)
        features_matmul(1, 1)
        weights_spread(1, 1)
        tanh(0, 1)
        weights_p(1)
        tanh(1, 1)
        moment(0, 0)
        product(0, 1)
        product(1, 1)

        def extra(s):
            if s == 1:
                w_interleave(2)
            if s == 2:
                w_quantize(2)
            if s in (3, 4, 5, 6):
                g, h = (s - 3) // 2, (s - 3) % 2
                x_transpose(0, g, h)
                x_copy(0, g, h)
            if s in (5, 7):
                x_quantize(0, (s - 5) // 2)
            if s in (6, 8):
                weights_spread(0, (s - 6) // 2)
            if s == 4:
                normaliser_a()
            if s == 6:
                normaliser_b()

        n_units = 2 * NB

        def part(what, s):
            if what == "x":
                extra(s)
            if what == "m" and s + 1 < n_units:
                features_matmul(s + 1, 0)
                features_matmul(s + 1, 1)
            if what == "t" and 1 < s < n_units:
                tanh(s, 0)
                tanh(s, 1)
            if what == "p" and 1 < s < n_units:
                product(s, 0)
                product(s, 1)
            if what in "ab" and 0 <= s - 1 < n_units and s - 1 + "ab".index(what) > 0:
                moment(s - 1, "ab".index(what))
                if what == "b" and NB <= s - 1 and (s % 2 == 0 or s - 1 == n_units - 2):
                    moment_total(0, s - 2 + s % 2 - NB if s < n_units else s - 1 - NB, s - NB)
                if what == "b" and s == NB:
                    moment_total(1, 0, NB)
            for d in (3, 2):
                if 0 <= s - d < n_units and d == int(OFF[s - d]):
                    if what == "r":
                        product_transpose(s - d)
                    if what == "g":
                        grouping(s - d)
            for d in (4, 3):
                if what == "q" and 0 <= s - d < n_units and d == int(OFF[s - d]) + 1:
                    quantize(s - d)
            if what == "1" and s == NB + 2:
                spread_m1(0)
                spread_m1(1)
            if what == "f":
                while waiting:
                    finish(*waiting.pop(0))
            for i in range(NB):
                lag_step = max(NB + LAG + i, max(NB + fb + int(OFF[NB + fb]) + 1 for fb in home[0, i][0]))
                if what == "1" and s == lag_step - 1:
                    rank_one(i)
                if what == "l" and s == lag_step:
                    for v in range(2):
                        if waiting:
                            finish(*waiting.pop(0))
                        lag_matmul(i, v)
                    waiting.extend([(i, 0), (i, 1)])

        waiting = []
        for s in range(1, n_units + 7):
            for what in STEP:
                part(what, s)
